import numpy as np, ml_dtypes
CORES = [9,25,41,57]
N = 4
BF = ml_dtypes.bfloat16
def gentries(a):
    return np.ascontiguousarray(a.reshape(8, 16, -1).transpose(0, 2, 1)).reshape(8, -1)
def gtable(e):
    e = np.asarray(e); return np.ascontiguousarray(e.reshape(8, -1, 16).transpose(0, 2, 1)).reshape(128, -1).astype(np.int32)
V, E, RO, TH = 4096, 512, 4, 8
S, M, F = 16 * N, RO * E, RO * E // N
U = np.arange(V)
ROOM = min(V // 2 - E, V // 20)
def graph(rng, full=()):
    A = np.full((8, 16, V), V, np.int64); place = np.argsort(rng.random((8, V)), axis=1)
    near = rng.random((8, 16)) < 0.7; near[np.arange(RO), np.arange(RO)] = True
    for g in full: near[g] = True
    for g in range(8):
        mk = np.argsort(rng.random((V // 32, 31)), axis=1)[:, :16] + 1
        for i in range(16):
            if near[g, i]:
                A[g, i, place[g]] = place[g][U ^ mk[U // 32, i]]
            else:
                o = rng.permutation(V); A[g, i, o[0::2]] = o[1::2]; A[g, i, o[1::2]] = o[0::2]
    return A, place
def thin(rng, A, most):
    for g in range(8):
        for i in range(16):
            p = A[g, i]; lo = np.nonzero((p < V) & (U < p) & (U > 0) & (p != V - 1))[0]
            d = rng.permutation(lo)[:int(rng.integers(0, most[i] + 1))]; e = p[d]
            A[g, i, d] = V; A[g, i, e] = V
    return A
def tests(rng, A, first, again):
    tv = np.zeros((8, RO, E), np.int64)
    for g in range(8):
        seen = np.zeros(V)
        for t in range(RO):
            p = A[g, t]; lo = np.nonzero((p < V) & (U < p))[0]
            key = rng.random(len(lo)) - first[g, lo] - first[g, p[lo]] - again * (seen[lo] + seen[p[lo]])
            lo = rng.permutation(lo[np.argsort(key)[:E]])
            tv[g, t] = np.where(rng.random(E) < 0.5, p[lo], lo)
            seen = np.zeros(V); seen[lo] = 1; seen[p[lo]] = 1
    return tv
def cloud(rng, place, lams):
    c = V // 32; n = lambda *s: rng.standard_normal(s, dtype=np.float32)
    lam = rng.choice(np.array(lams, np.float32), (8, 1, c, 1)); ld = (rng.random((8, 1, c, 32)) * 2 - 1).astype(np.float32)
    w = 128 + 25 * n(8, S, c, 1) + 60 * lam * ld * n(8, S, c, 1) + 20 * n(8, S, c, 32)
    w = np.clip(np.rint(w), 0, 255).astype(np.int64).reshape(8, S, V)
    step = rng.choice(np.array([1, 1, 1, 16, 64]), (8, 1, V)); w = w // step * step
    return np.take_along_axis(w, np.argsort(place, axis=1)[:, None, :], 2)
def pack(s, A, tv):
    return {"x": np.ascontiguousarray(s.reshape(8, N, 16, V).transpose(1, 0, 2, 3)).reshape(N, 128, V).astype(np.float32).astype(BF),
            "adj": np.stack([A.reshape(128, V).astype(np.int32)] * N), "tv": np.stack([gtable(tv.reshape(8, M))] * N)}
def setup_inputs(rng):
    A, place = graph(rng); A = thin(rng, A, [ROOM] * 16)
    return pack(cloud(rng, place, [0, 0, 0.3, 1]), A, tests(rng, A, np.zeros((8, V)), 0))
def setup_inputs_edge(rng):
    A, place = graph(rng); A = thin(rng, A, [ROOM] * 16)
    ty = rng.random((8, 1, V)); low = ty < 0.2; high = (ty >= 0.2) & (ty < 0.4)
    lv = np.where(low, rng.integers(40, 110, (8, 1, V)), rng.integers(190, 240, (8, 1, V)))
    goal = rng.choice(np.array([TH, TH - 1, -TH, 1 - TH] + [TH + 1] * 8 + [-TH - 1] * 8 + [TH + 2] * 4 + [-TH - 2] * 4 + [S - 2] * 2), (8, 1, V))
    tie = (S - goal) % 2; nb = (S - tie - goal) // 2
    o = np.argsort(np.argsort(rng.random((8, S - 1, V), dtype=np.float32), axis=1), axis=1)
    run = rng.random((8, 1, V)); k = np.arange(S - 1)[None, :, None]
    o = np.where(run < 0.35, S - 2 - k, np.where(run < 0.6, k, o))
    out = np.where(rng.random((8, S - 1, V), dtype=np.float32) < 0.5, 10, 250)
    rest = np.where(low | high, lv, np.where(o < nb, 150, out))
    head = np.where(low, 100, np.where(high, lv, np.where(tie == 1, 100, 250)))
    s = np.concatenate([head, rest], axis=1)
    return pack(s, A, tests(rng, A, (low | high)[:, 0].astype(np.float64), 0))
def setup_inputs_alike(rng):
    A, place = graph(rng, (0, 6, 7)); o = place[7, :32 * (V // 128)]; A[7][:, o] = A[7, 0, o]
    A = thin(rng, A, [ROOM] * 16); A[1::2, 8:] = A[1::2, :8]
    A[::6, 1] = A[::6, 0]; A[6, 9:] = A[6, 8]
    s = cloud(rng, place, [0, 0.3, 1]); s[2:6] = 255 * (rng.random((4, S, V)) < 0.5)
    for g in (0, 7):
        p = A[g, 15]; lo = np.nonzero((p < V) & (U < p))[0]; lo = rng.permutation(lo)[:V // 20]; s[g][:, p[lo]] = s[g][:, lo]
    return pack(s, A, tests(rng, A, np.zeros((8, V)), 0))
def setup_inputs_bare(rng):
    A, place = graph(rng); A = thin(rng, A, [ROOM] * RO + [V // 2] * (16 - RO))
    A[1, RO:15] = V; A[2, RO:] = V; A[6, RO + 1:] = V
    s = cloud(rng, place, [0, 0, 0.3, 1]); first = np.zeros((8, V)); first[:, 0] = 1; first[:, V - 1] = 1
    for g in range(8):
        for c in (0, V - 1):
            y = int(A[g, RO, c])
            if y < V:
                s[g][:, c] = s[g][:, y]; first[g, y] = 1
    return pack(s, A, tests(rng, A, first, 0))
def setup_inputs_chain(rng):
    A, place = graph(rng, (5, 6)); A = thin(rng, A, [ROOM] * 16)
    s = cloud(rng, place, [0.3, 0.6, 1])
    s[5] = rng.integers(0, 256, (S, 1))
    s[6] = rng.integers(0, 256, (S, V)); p = A[6, 1]; lo = np.nonzero((p < V) & (U < p))[0]; s[6][:, p[lo]] = s[6][:, lo]
    return pack(s, A, tests(rng, A, np.zeros((8, V)), 1))
def setup_inputs_spread(rng):
    A, place = graph(rng); A = thin(rng, A, [ROOM] * 16)
    s = np.floor(np.exp2(8 * rng.random((8, 1, V))) * rng.random((8, S, V))) * (rng.random((8, 1, V)) > 0.0625)
    return pack(s.astype(np.int64), A, tests(rng, A, np.zeros((8, V)), 0))
def check_inputs(d):
    bad = []; xf = d["x"].astype(np.float32)
    if not np.all((xf >= 0) & (xf <= 255) & (np.floor(xf) == xf)): bad.append("range of x")
    for k, hi in (("adj", V), ("tv", V - 1)):
        if np.min(d[k]) < 0 or np.max(d[k]) > hi: bad.append("range of " + k)
        if np.any(d[k] != d[k][:1]): bad.append(k + " alike on all ranks")
    if "range of adj" in bad or "range of tv" in bad: return bad
    A = d["adj"][0].astype(np.int64).reshape(8, 16, V); B = np.concatenate([A, np.full((8, 16, 1), V, np.int64)], axis=2)
    if not np.all((A == V) | ((np.take_along_axis(B, A, 2) == U) & (A != U))): bad.append("partners are mutual")
    vs = gentries(d["tv"][0]).astype(np.int64).reshape(8, RO, E); g8 = np.arange(8)[:, None]
    for t in range(RO):
        v = vs[:, t]; y = A[g8, t, v]; both = np.sort(np.concatenate([v, y], axis=1), axis=1)
        if np.any(y >= V) or np.any(both[:, 1:] == both[:, :-1]): bad.append("ends of round " + str(t))
    return bad
def reference(x, adj, tv):
    A = adj[0].astype(np.int64).reshape(8, 16, V)
    s = np.ascontiguousarray(x.astype(np.float32).astype(np.int32).reshape(N, 8, 16, V).transpose(1, 0, 2, 3)).reshape(8, S, V)
    vs = gentries(tv[0]).astype(np.int64).reshape(8, RO, E); ys = np.zeros((8, RO, E), np.int64); sp = np.full((8, RO, E), V, np.int64)
    g8 = np.arange(8)[:, None]; g3 = np.arange(8)[:, None, None]; i3 = np.arange(16)[None, :, None]
    for t in range(RO):
        v = vs[:, t]; y = A[g8, t, v]; ys[:, t] = y
        z = A[g3, i3, y[:, None, :]]
        zz = np.where(z < V, z, 0); a = np.zeros((8, 16, E), np.int64)
        xv = np.take_along_axis(s, v[:, None, :], 2); xy = np.take_along_axis(s, y[:, None, :], 2)
        for i in range(16):
            xz = np.take_along_axis(s, zz[:, i][:, None, :], 2)
            a[:, i] = np.sum(np.sign((xv - xz) * (xy - xz)), axis=1)
        ok = (z < V) & (z != v[:, None, :]) & (np.abs(a) <= TH)
        hit = np.any(ok, axis=1); i1 = np.argmax(ok, axis=1)
        sp[:, t] = np.where(hit, np.take_along_axis(z, i1[:, None, :], 1)[:, 0], V)
        A[g8, t, v] = np.where(hit, V, y); A[g8, t, y] = np.where(hit, V, v)
    v = vs.reshape(8, 1, M); y = ys.reshape(8, 1, M); se = sp.reshape(8, 1, M)
    w = A[g3, i3, y]; ww = np.where(w < V, w, 0); inside = np.zeros((8, 16, M), bool)
    for i in range(16): inside = inside | (A[g3, i, ww] == v)
    fl = (se < V) & (w < V) & inside & (w != se)
    return {"ysep": np.stack([sp.reshape(8, M)] * N).astype(np.float32),
            "yflag": np.stack([fl[:, :, r * F:(r + 1) * F].reshape(128, F) for r in range(N)]).astype(np.float32).astype(BF)}

@@ -1,0 +1,522 @@
+from concourse.bass import DstId, RemoteDMATransfer
+from concourse.mybir import AluOpType as OP, ActivationFunctionType as AF
+
+NR, E = 4, 512
+ND = 4
+BF, U2, F4, F2, I4 = "bfloat16", "uint16", "float32", "float16", "int32"
+SCRATCH = {}
+for _n, _w, _d in (
+        ("adjs", 4096, I4), ("xs", 4112, BF), ("tvs", 128, I4), ("tvu", 128, U2), ("iot", 4096, I4), ("ones", 128, BF),
+        ("c1", 8, BF), ("c2", 8, BF), ("b1", 128, BF), ("bm", 128, BF), ("im", 128, BF), ("lt", 128, BF), ("q16", 128, BF),
+        ("qm", 128, BF), ("hi", 128, BF), ("nhi", 128, BF), ("ni", 128, BF), ("pi", 128, BF), ("pn", 128, BF),
+        ("nbm", 128, F2), ("b2k", 128, F2), ("bcb", 2048, BF), ("bch", 2048, F2), ("gall", 2048, BF), ("gp", 512, BF),
+        ("gn", 512, BF), ("ve", 512, U2), ("vj", 32, U2), ("cvj", 512, U2), ("lv", 128, U2), ("lvi", 128, I4), ("vli", 32, I4),
+        ("mvi", 128, I4), ("mv", 128, U2), ("cvl", 512, F2), ("w4", 512, F4), ("mt_", 8192, BF), ("base", 512, BF),
+        ("eqs", 512, BF), ("nh", 512, BF), ("fl", 512, BF), ("wsum", 128, BF), ("ok", 128, BF), ("first", 128, F2),
+        ("fz", 128, F2), ("tj", 128, U2), ("tl", 128, U2), ("mint", 512, U2), ("eq", 2048, BF), ("inv", 2048, BF),
+        ("lki", 512, I4), ("yli", 128, I4), ("mini", 512, I4), ("ce", 2048, U2), ("cj", 2048, U2), ("yj", 2048, U2),
+        ("li", 2048, U2), ("zc", 2048, F2), ("h", 16384, BF), ("part", 2048, BF), ("pin", 2048, BF), ("sepin", 2048, F4),
+        ("sepf", 2048, F4), ("rv", 2048, BF), ("mg", 2048, BF), ("rk", 8192, BF), ("xv", 1024, BF), ("xy", 1024, BF),
+        ("m", 2048, F4), ("hh", 1024, BF), ("d", 1024 * ND, BF), ("w", 3072, BF), ("s", 3072, BF)):
+    SCRATCH[_n] = ("sbuf", [128, _w], _d)
+for _n, _w in (("psT", 2048), ("psA", 512), ("psX", 512), ("psY", 512), ("psZ", 512)):
+    SCRATCH[_n] = ("psum", [128, _w], F4)
+
+SEMAPHORES = ["cv", "ca", "cp", "cg", "ltv", "ladj", "lx", "loc", "svj", "slv", "oflag"]
+for _t in range(NR):
+    SEMAPHORES += ["%s%d" % (_k, _t) for _k in ("arr", "sar", "stj", "stl", "osep")] + ["sli%d_%d" % (_t, _k) for _k in range(5)]
+
+CY = 1e-3
+GA, SC, PE = 1.5, 3.6, 0.5e-3
+WAKE = 0.1
+
+
+def rank_program(g, core, T, topo):
+    r = T.rank_of(core)
+    if r is None:
+        return
+    eng = {"v": g.vector, "a": g.scalar, "p": g.tensor, "g": g, "s": g.sync}
+    tasks = []
+
+    def op(e, fn, reads, writes, cost):
+        tasks.append((e, "op", fn, "c" + e, 1, reads, writes, cost, cost))
+
+    def dma(e, sem, out, in_, reads, writes, lat=2.2):
+        tasks.append((e, "dma", lambda q: q.dma_start(out, in_), sem, 16, reads, writes, 0.1, lat))
+
+    def ap(rg):
+        return T[rg[0]][:, rg[1]:rg[2]]
+
+    def full(name):
+        return (name, 0, SCRATCH[name][1][1])
+
+    def blk(name, k, w=512):
+        return (name, w * k, w * k + w)
+
+    def part(rg, q, n=4):
+        w = (rg[2] - rg[1]) // n
+        return (rg[0], rg[1] + q * w, rg[1] + q * w + w)
+
+    def small(*rgs):
+        return all(SCRATCH[x[0]][0] == "sbuf" and SCRATCH[x[0]][2] in (BF, U2, F2) for x in rgs)
+
+    def vc(n, f=1.0):
+        return 0.05 + max(64, n * f) * CY
+
+    def copy(e, out, in_):
+        n = in_[2] - in_[1]
+        if e == "v":
+            op("v", lambda q: q.tensor_copy(ap(out), ap(in_)), [in_], [out], vc(n, 0.5 if small(out, in_) else 1))
+        else:
+            op("a", lambda q: q.activation(ap(out), ap(in_), AF.Copy), [in_], [out], 0.15 + n * CY)
+
+    def act(out, in_, func):
+        op("a", lambda q: q.activation(ap(out), ap(in_), func), [in_], [out], 0.15 + (in_[2] - in_[1]) * CY)
+
+    def tt(out, a, b, o):
+        f = 1 if a[0].startswith("ps") or b[0].startswith("ps") else 2
+        op("v", lambda q: q.tensor_tensor(ap(out), ap(a), ap(b), o), [a, b], [out], vc(a[2] - a[1], f))
+
+    def ts(out, a, s1, o1):
+        op("v", lambda q: q.tensor_scalar(ap(out), ap(a), s1, None, o1), [a], [out], vc(a[2] - a[1], 0.5 if small(out, a) else 1))
+
+    def gcost(off):
+        return 0.07 + 16 * (off[2] - off[1]) * GA * CY
+
+    def gather(e, out, win, off):
+        if e == "v":
+            op("v", lambda q: q.tensor_copy(ap(out), ap(win).indirect(ap(off))), [win, off], [out], gcost(off))
+        else:
+            op("a", lambda q: q.activation(ap(out), ap(win).indirect(ap(off)), AF.Copy), [win, off], [out], gcost(off))
+
+    def gather_less(out, win, off):
+        op("v", lambda q: q.tensor_scalar(ap(out), ap(win).indirect(ap(off)), -2048.0, None, OP.add), [win, off], [out], gcost(off))
+
+    def mm(out, lhs, rhs, start, stop):
+        op("p", lambda q: q.matmul(ap(out), ap(lhs), ap(rhs), start, stop), [lhs, rhs], [out], 0.03 + (rhs[2] - rhs[1]) * PE)
+
+    def gi(i):
+        return blk("gall", i, 128)
+
+    def tj(t):
+        return blk("tj", t, 32)
+
+    def tl(t):
+        return blk("tl", t, 32)
+
+    def li(t, i, n=1):
+        return ("li", 512 * t + 32 * i, 512 * t + 32 * i + 32 * n)
+
+    def hw(t):
+        return blk("h", t, 4096)
+
+    XW, AW, IW = full("xs"), full("adjs"), full("iot")
+
+    dma("s", "ltv", T.tvs[:, :], T.tv[:, :], [], [full("tvs")])
+    dma("s", "ladj", T.adjs[:, :], T.adj[:, :], [], [full("adjs")], 9.0)
+    dma("s", "lx", T.xs[:, 0:4096], T.x[:, :], [], [("xs", 0, 4096)], 13.0)
+
+    def fill(rg, val, cost):
+        op("v", lambda q: q.memset(ap(rg), val), [], [rg], cost)
+
+    fill(full("ones"), 1.0, 0.1)
+    fill(full("bcb"), 1.0, 1.0)
+    fill(full("gall"), 0.0, 1.0)
+    fill(("xs", 4096, 4112), 0.0, 0.1)
+
+    def asel(out, in_, pat, cmp, base, cm):
+        op("g", lambda q: q.affine_select(ap(out), ap(in_), pat, cmp, 0.0, base, cm), [in_], [out], 0.2 + 2 * CY * (in_[2] - in_[1]))
+
+    one128 = full("ones")
+    op("g", lambda q: q.iota(T.iot[:, :], [[1, 4096]], 0, 0), [], [full("iot")], 8.2)
+    asel(full("c1"), ("ones", 0, 8), [[-16, 8]], OP.is_ge, 0, 1)
+    asel(full("c2"), full("c1"), [[16, 8]], OP.is_ge, 15, -1)
+    asel(full("im"), one128, [[-1, 128]], OP.is_equal, 0, 1)
+    asel(full("b1"), one128, [[-16, 8], [0, 16]], OP.is_ge, 0, 1)
+    asel(full("bm"), full("b1"), [[16, 8], [0, 16]], OP.is_ge, 15, -1)
+    asel(full("lt"), full("bm"), [[1, 128]], OP.is_gt, 0, -1)
+    asel(full("bcb"), full("bcb"), [[-1, 16], [-16, 8], [0, 16]], OP.is_equal, 0, 1)
+
+    def zeros(s):
+        op("g", lambda q: q.iota(ap(hw(s)), [[0, 4096]], 0, 0, allow_small_or_imprecise_dtypes=True), [], [hw(s)], 8.2)
+
+    for s in range(NR if r != 3 else 3):
+        zeros(s)
+
+    def diag(i):
+        op("v", lambda q: q.tensor_copy(T.gall[:, 128 * i + i:128 * i + 128:16], T.c2[:, :]), [full("c2")], [gi(i)], 0.12)
+
+    copy("v", full("tvu"), full("tvs"))
+    for i in range(16):
+        diag(i)
+    for nm, f in (("hi", 0.5), ("nhi", -0.5), ("ni", -1.0), ("pi", 512.0), ("pn", -512.0)):
+        ts(full(nm), full("im"), f, OP.mult)
+    ts(full("gp"), ("gall", 0, 512), 64.0, OP.mult)
+    ts(full("gn"), ("gall", 0, 512), -64.0, OP.mult)
+
+    def rows_v(t):
+        gather("v", blk("ce", t), AW, blk("tvu", t, 32))
+        dma("s", "stj%d" % t, ap(tj(t)), T.ce[t::16, 512 * t:512 * t + 512], [blk("ce", t)], [tj(t)])
+
+    def rows_y(t):
+        gather("v", blk("cj", t), AW, tj(t))
+        gather("v", blk("yj", t), IW, tj(t))
+        dma("s", "sli%d_4" % t, ap(li(t, t)), T.cj[t::16, 512 * t:512 * t + 512], [blk("cj", t)], [li(t, t)], 2.4)
+        dma("s", "stl%d" % t, ap(tl(t)), T.yj[0::16, 512 * t:512 * t + 512], [blk("yj", t)], [tl(t)])
+        for n, i in enumerate([i for i in range(16) if i != t]):
+            dma("s" if n % 2 or t else "a", "sli%d_%d" % (t, n // 4), ap(li(t, i)), T.cj[i::16, 512 * t:512 * t + 512],
+                [blk("cj", t)], [li(t, i)], 2.5 + 0.3 * n)
+
+    for t in range(NR):
+        rows_v(t)
+    for t in range(NR):
+        rows_y(t)
+
+    def prep(t):
+        b = t % 2
+        xv, xy, hb = blk("xv", b), blk("xy", b), blk("hh", b)
+        gather("a", xy, XW, tl(t))
+        gather("a", xv, XW, li(t, t))
+        mm(full("psX"), full("hi"), xv, True, False)
+        mm(full("psX"), full("hi"), xy, False, True)
+        mm(full("psY"), full("hi"), xv, True, False)
+        mm(full("psY"), full("nhi"), xy, False, True)
+        copy("a", blk("m", 2 * b), full("psX"))
+        copy("a", blk("m", 2 * b + 1), full("psX"))
+        act(hb, full("psY"), AF.Abs)
+
+    def mins(t):
+        lk, yl, mn = blk("lki", t, 128), blk("yli", t, 32), blk("mini", t, 128)
+        copy("v", lk, ("li", 512 * t, 512 * t + 128))
+        copy("v", yl, tl(t))
+        for s in range(NR):
+            tt(blk("mini", 4 * t + s, 32), blk("lki", 4 * t + s, 32), yl, OP.min)
+        copy("v", blk("mint", t, 128), mn)
+
+    def cols(t):
+        zc, inv, eq, off = blk("zc", t), blk("inv", t), blk("eq", t), tl(t)
+        if t != r:
+            zc, inv, off = part(zc, r), part(inv, r), part(off, r)
+        gather_less(zc, AW, off)
+        ts(inv, zc, 2048.0, OP.is_equal)
+        zq = part(blk("zc", t), r)
+        mm(("psZ", 0, 128), blk("bch", t, 128), zq, True, True)
+        tt(part(eq, r), ("psZ", 0, 128), zq, OP.is_equal)
+
+    def bigmats():
+        copy("v", full("bch"), full("bcb"))
+        ts(full("q16"), full("lt"), 16.0, OP.mult)
+        ts(full("nbm"), full("bm"), -1.0, OP.mult)
+        ts(full("b2k"), full("bm"), 2048.0, OP.mult)
+        tt(full("qm"), full("q16"), full("im"), OP.subtract)
+
+    units = []
+    for t in range(NR):
+        ent = [i for i in range(16) if i != t]
+        us = []
+        k = 0
+        while k < len(ent):
+            n = 2 if k + 1 < len(ent) and ent[k + 1] == ent[k] + 1 else 1
+            us.append((t, ent[k], n))
+            k += n
+        for j, u in enumerate(us):
+            units.append(u + (j == 0, j == len(us) - 1))
+
+    def unit(n):
+        t, i, k, fst, lst = units[n]
+        c, d0, w0, p0, m0 = 512 * k, 1024 * (n % ND), 1024 * (n % 3), 1024 * (n % 2), 1024 * (t % 2)
+        d, w, s, m, off = ("d", d0, d0 + c), ("w", w0, w0 + c), ("s", w0, w0 + c), ("m", m0, m0 + c), li(t, i, k)
+        op("v", lambda q: q.tensor_tensor(ap(d), ap(XW).indirect(ap(off)), ap(m), OP.subtract), [XW, off, m], [d], gcost(off))
+        act(w, d, AF.Abs)
+        for j in range(k):
+            o = ("psT", p0 + 512 * j, p0 + 512 * j + 512)
+            mm(o, full("im"), ("w", w0 + 512 * j, w0 + 512 * j + 512), True, False)
+            mm(o, full("ni"), blk("hh", t % 2), False, True)
+        act(s, ("psT", p0, p0 + c), AF.Sign)
+        for j in range(k):
+            mm(full("psA"), gi(i + j), ("s", w0 + 512 * j, w0 + 512 * j + 512), fst and j == 0, lst and j == k - 1)
+
+    others = [q for q in range(NR) if q != r]
+    links = topo.engines(core, T.cores[others[0]])
+
+    def dst(q):
+        a = topo.addr(T.cores[q])
+        return DstId(rid=a[0], pnc=a[1])
+
+    def remote(name, t, transfers, nloc, nrem, src, land):
+        tasks.append(("g", "send", lambda q: q.remote_dma_fused(transfers, local_sem=T.sem.loc), "loc", nloc, [src],
+                      [("token" + name, t, t + 1)], 0.6, 0.6))
+        tasks.append((None, "land", None, name + str(t), 3 * nrem, [("token" + name, t, t + 1)], land, 0.0, 4.5))
+
+    def share(t):
+        mine = blk("part", t)
+        copy("a", mine, full("psA"))
+        k = len(links) // 4
+        tr = []
+        for n, q in enumerate(others):
+            mask = sum(1 << e for e in links[n * k:n * k + k])
+            tr.append(RemoteDMATransfer(dst_ids=[dst(q)], dma_engine_mask=mask, remote_sem=T.sem["arr%d" % t],
+                                        srcs=[ap(part(mine, q))], dsts=[ap(part(blk("pin", t), r))]))
+        remote("arr", t, tr, 3 * k, k, mine, [part(blk("pin", t), q) for q in others])
+
+    def rk(t, s):
+        return blk("rk", 4 * t + s)
+
+    def mi(t, s):
+        return blk("mint", 4 * t + s, 32)
+
+    def look(e, t, s):
+        if t == r:
+            gather(e, rk(t, s), hw(s), mi(t, s))
+        else:
+            gather(e, part(rk(t, s), r), hw(s), part(mi(t, s), r))
+
+    def decide(t):
+        X, Y = ("psX", 0, 128), ("psY", 0, 128)
+        mm(X, full("pi"), part(blk("eq", t), r), True, False)
+        mm(X, full("pi"), part(blk("inv", t), r), False, False)
+        for s in range(t):
+            mm(X, blk("gp", s, 128), part(rk(t, s), r), False, False)
+        mm(X, full("im"), part(blk("part", t), r), False, False)
+        for q in others:
+            mm(X, full("im"), part(blk("pin", t), q), False, q == others[-1])
+        act(full("wsum"), X, AF.Abs)
+        ts(full("ok"), full("wsum"), 8.0, OP.is_le)
+        mm(X, full("qm"), full("ok"), True, True)
+        ts(full("first"), X, -1.0, OP.is_equal)
+        tt(full("fz"), full("first"), part(blk("zc", t), r), OP.mult)
+        mm(Y, full("b2k"), full("first"), True, False)
+        mm(Y, full("nbm"), full("fz"), False, True)
+        mine = part(blk("sepin", t), r)
+        copy("a", mine, Y)
+        tr = [RemoteDMATransfer(dst_ids=[dst(q) for q in others], dma_engine_mask=topo.mask(core, T.cores[others[0]]),
+                                remote_sem=T.sem["sar%d" % t], srcs=[ap(mine)], dsts=[ap(mine) for _ in others])]
+        remote("sar", t, tr, len(links), len(links), mine, [part(blk("sepin", t), q) for q in others])
+
+    def mark(t):
+        if t == 3 and r == 3:
+            return
+        off, src = mi(t, t), blk("sepin", t)
+        op("v", lambda q: q.tensor_copy(ap(hw(t)).indirect(ap(off)), ap(src)), [off, src], [hw(t)], 0.07 + 512 * SC * CY)
+
+    def seps(t):
+        a, b = 512 * t, 512 * t + 512
+        for n in range(2):
+            half(a + n, b, part(blk("sepin", t), n, 2), ("sepf", a, b))
+        dma("s", "osep%d" % t, T.ysep[:, a:b], T.sepf[0::16, a:b], [("sepf", a, b)], [])
+
+    def half(a, b, src, out):
+        op("a", lambda q: q.activation(T.sepf[:, a:b:2], ap(src), AF.Identity, bias=4096.0, scale=-1.0), [src], [out], 0.4)
+
+    def mj(j):
+        return blk("mt_", j)
+
+    def fl_static():
+        gather("v", full("ve"), IW, blk("tvu", r, 32))
+        dma("s", "svj", T.vj[:, :], T.ve[0::16, :], [full("ve")], [full("vj")])
+        gather("v", full("cvj"), AW, full("vj"))
+        for s in range(NR):
+            dma("s", "slv", ap(blk("lv", s, 32)), T.cvj[s::16, :], [full("cvj")], [blk("lv", s, 32)])
+        gather_less(full("cvl"), AW, li(r, r))
+        op("v", lambda q: q.tensor_scalar(T.w4[:, :], ap(blk("zc", r)), -1.0, 2048.0, OP.mult, OP.add), [blk("zc", r)], [full("w4")], vc(512))
+        copy("v", full("lvi"), full("lv"))
+        copy("v", full("vli"), li(r, r))
+        for s in range(NR):
+            tt(blk("mvi", s, 32), blk("lvi", s, 32), full("vli"), OP.min)
+        copy("v", full("mv"), full("mvi"))
+        for j in range(16):
+            if j != r:
+                mm(full("psZ"), blk("bch", j, 128), full("cvl"), True, True)
+                tt(mj(j), full("psZ"), blk("zc", r), OP.is_equal)
+        Z = full("psZ")
+        mm(Z, full("pn"), blk("inv", r), True, False)
+        for j in range(4, 16):
+            mm(Z, full("im"), mj(j), False, j == 15)
+        copy("a", full("base"), Z)
+
+    def fl_own():
+        tt(full("eqs"), blk("sepin", r), full("w4"), OP.is_equal)
+        ts(full("nh"), blk("sepin", r), 0.0, OP.is_equal)
+
+    def fl_round(e, s):
+        if s != r:
+            gather(e, blk("rv", s), hw(s), blk("mv", s, 32))
+            if s > r:
+                look(e, r, s)
+            tt(blk("mg", s), mj(s), blk("rv", s), OP.is_gt)
+
+    prep(0)
+    bigmats()
+    cols(r)
+    per = len(units) // NR
+    for t in range(NR):
+        if t:
+            prep(t)
+        mins(t)
+        if t != r:
+            cols(t)
+        for n in range(per):
+            unit(per * t + n)
+            if t and n == 2:
+                for s in range(t - 1):
+                    look("v", t, s)
+                decide(t - 1)
+            if t and n == 5:
+                mark(t - 1)
+                look("v", t, t - 1)
+                seps(t - 1)
+                if t - 1 == r:
+                    fl_own()
+                fl_round("v", t - 1)
+        if t == 0:
+            fl_static()
+        share(t)
+    F = full("psA")
+    mm(F, full("im"), full("base"), True, False)
+    for s in range(3):
+        if s != r:
+            mm(F, full("im"), blk("mg", s), False, False)
+            mm(F, blk("gn", s, 128), rk(r, s), False, False)
+    if r != 3:
+        mm(F, full("pn"), full("eqs"), False, False)
+        mm(F, full("pn"), full("nh"), False, False)
+    decide(3)
+    mark(3)
+    if r != 3:
+        fl_round("a", 3)
+        mm(F, blk("gn", 3, 128), rk(r, 3), False, False)
+        mm(F, full("im"), blk("mg", 3), False, True)
+    else:
+        fl_own()
+        mm(F, full("pn"), full("nh"), False, False)
+        mm(F, full("pn"), full("eqs"), False, True)
+    seps(3)
+    op("v", lambda q: q.tensor_scalar(T.fl[:, 0::2], T.psA[:, 0:256], 0.0, None, OP.is_gt), [F], [full("fl")], 0.3)
+    op("v", lambda q: q.tensor_scalar(T.fl[:, 1::2], T.psA[:, 256:512], 0.0, None, OP.is_gt), [F], [full("fl")], 0.3)
+    dma("s", "oflag", T.yflag[:, :], T.fl[:, :], [full("fl")], [])
+
+    cnt, snap, recs = {}, {}, {}
+    clock = {e: {} for e in eng}
+
+    def wait(e, sem, val, isdma):
+        if isdma:
+            val = cnt[sem]
+        if clock[e].get(sem, 0) >= val:
+            return
+        eng[e].wait_ge(T.sem[sem], val)
+        for k, v in snap.get(sem if isdma else (sem, val), {}).items():
+            if clock[e].get(k, 0) < v:
+                clock[e][k] = v
+        clock[e][sem] = max(clock[e].get(sem, 0), val)
+
+    for x in schedule(tasks):
+        e, kind, fn, sem, inc, reads, writes, _, _ = tasks[x]
+        reads = [q for q in reads if not q[0].startswith("token")]
+        writes = [q for q in writes if not q[0].startswith("token")]
+        isdma = kind != "op"
+        if kind != "land":
+            best = {}
+            for isw, rgs in ((False, reads), (True, writes)):
+                for buf, a, b in rgs:
+                    for c0, c1, w, e2, s2, v2, d2 in recs.get(buf, []):
+                        if c0 >= b or a >= c1:
+                            continue
+                        if not isw and not w and not (buf.startswith("ps") and e2 != e):
+                            continue
+                        if isw and e2 == e and not d2 and not isdma and (not w or e == "p"):
+                            continue
+                        if s2 not in best or best[s2][0] < v2:
+                            best[s2] = (v2, d2)
+            for s2 in sorted(best, key=lambda z: (best[z][1], z)):
+                wait(e, s2, best[s2][0], best[s2][1])
+        cnt[sem] = cnt.get(sem, 0) + inc
+        if kind == "send":
+            fn(eng[e])
+            continue
+        if kind != "land":
+            fn(eng[e]).then_inc(T.sem[sem], inc)
+            if kind == "op":
+                sn = dict(clock[e])
+                sn[sem] = cnt[sem]
+                snap[(sem, cnt[sem])] = sn
+            else:
+                sn = snap.setdefault(sem, {})
+                for k, v in clock[e].items():
+                    sn[k] = max(sn.get(k, 0), v)
+        for buf, a, b in writes:
+            lst = recs.setdefault(buf, [])
+            lst[:] = [q for q in lst if not (a <= q[0] and q[1] <= b)]
+            lst.append((a, b, True, e, sem, cnt[sem], isdma))
+        for buf, a, b in reads:
+            lst = recs.setdefault(buf, [])
+            lst[:] = [q for q in lst if not (not q[2] and q[4] == sem and a <= q[0] and q[1] <= b)]
+            lst.append((a, b, False, e, sem, cnt[sem], isdma))
+
+    for sem, val in cnt.items():
+        if clock["g"].get(sem, 0) < val:
+            g.wait_ge(T.sem[sem], val)
+            clock["g"][sem] = val
+
+
+def schedule(tasks):
+    n = len(tasks)
+    deps = [set() for _ in range(n)]
+    recs, group = {}, {}
+    for x in range(n):
+        e, kind, _, sem, _, reads, writes, _, _ = tasks[x]
+        for isw, rgs in ((False, reads), (True, writes)):
+            for buf, a, b in rgs:
+                for c0, c1, w, e2, y in recs.get(buf, []):
+                    if c0 < b and a < c1 and (isw or w or (buf.startswith("ps") and e2 != e)):
+                        deps[x].add(y)
+        for y in list(deps[x]):
+            if tasks[y][1] == "dma":
+                deps[x].update(z for z in group[tasks[y][3]] if z < x)
+        if kind == "dma":
+            group.setdefault(sem, []).append(x)
+        for buf, a, b in writes:
+            lst = recs.setdefault(buf, [])
+            lst[:] = [q for q in lst if not (a <= q[0] and q[1] <= b)]
+            lst.append((a, b, True, e, x))
+        for buf, a, b in reads:
+            recs.setdefault(buf, []).append((a, b, False, e, x))
+        deps[x].discard(x)
+    succ = [[] for _ in range(n)]
+    for x in range(n):
+        for y in deps[x]:
+            succ[y].append(x)
+    prio = [0.0] * n
+    for x in range(n - 1, -1, -1):
+        prio[x] = tasks[x][8] + WAKE + max([prio[y] for y in succ[x]], default=0.0)
+    left = [len(deps[x]) for x in range(n)]
+    at = [0.0] * n
+    free = {}
+    ready = {}
+    for x in range(n):
+        if not left[x]:
+            ready.setdefault(tasks[x][0], []).append(x)
+    order = []
+    while len(order) < n:
+        pick = None
+        for e in sorted(ready, key=str):
+            lst = ready[e]
+            if not lst:
+                continue
+            f = free.get(e, 0.0)
+            s0 = min(max(f, at[x]) for x in lst)
+            if pick is None or s0 < pick[0]:
+                pick = (s0, e)
+        s0, e = pick
+        x = max((y for y in ready[e] if max(free.get(e, 0.0), at[y]) <= s0 + 0.05), key=lambda y: (prio[y], -y))
+        ready[e].remove(x)
+        st = max(free.get(e, 0.0), at[x])
+        if e is not None:
+            free[e] = st + tasks[x][7]
+        end = st + tasks[x][8] + WAKE
+        order.append(x)
+        for y in succ[x]:
+            at[y] = max(at[y], end)
+            left[y] -= 1
+            if not left[y]:
+                ready.setdefault(tasks[y][0], []).append(y)
+    return order

@@ -15,7 +15,7 @@ for _n, _w, _d in (
         ("eqs", 512, BF), ("nh", 512, BF), ("fl", 512, BF), ("wsum", 128, BF), ("ok", 128, BF), ("first", 128, F2),
         ("fz", 128, F2), ("tj", 128, U2), ("tl", 128, U2), ("mint", 512, U2), ("eq", 2048, BF), ("inv", 2048, BF),
         ("lki", 512, I4), ("yli", 128, I4), ("mini", 512, I4), ("ce", 2048, U2), ("cj", 2048, U2), ("yj", 2048, U2),
-        ("li", 2048, U2), ("zc", 2048, F2), ("h", 16384, BF), ("part", 2048, BF), ("pin", 2048, BF), ("sepin", 2048, F4),
+        ("li", 2048, U2), ("zc", 2048, F2), ("h", 16384, BF), ("part", 2048, BF), ("pin", 2048, BF), ("sepin", 2048, U2),
         ("sepf", 2048, F4), ("rv", 2048, BF), ("mg", 2048, BF), ("rk", 8192, BF), ("xv", 1024, BF), ("xy", 1024, BF),
         ("m", 2048, F4), ("hh", 1024, BF), ("d", 1024 * ND, BF), ("w", 3072, BF), ("s", 3072, BF)):
     SCRATCH[_n] = ("sbuf", [128, _w], _d)
@@ -26,9 +26,9 @@ SEMAPHORES = ["cv", "ca", "cp", "cg", "ltv", "ladj", "lx", "loc", "svj", "slv", 
 for _t in range(NR):
     SEMAPHORES += ["%s%d" % (_k, _t) for _k in ("arr", "sar", "stj", "stl", "osep")] + ["sli%d_%d" % (_t, _k) for _k in range(5)]
 
-CY = 1e-3
-GA, SC, PE = 1.5, 3.6, 0.5e-3
-WAKE = 0.1
+CY, GA, SC, PE = 0.9e-3, 1.55, 3.6, 0.43e-3
+WAKE, LAT = 0.05, 2.2
+LAND = {"arr": 4.0, "sar": 6.5}
 
 
 def rank_program(g, core, T, topo):
@@ -37,11 +37,14 @@ def rank_program(g, core, T, topo):
         return
     eng = {"v": g.vector, "a": g.scalar, "p": g.tensor, "g": g, "s": g.sync}
     tasks = []
+    bonus, lift = {}, [0.0]
 
     def op(e, fn, reads, writes, cost):
+        bonus[len(tasks)] = lift[0]
         tasks.append((e, "op", fn, "c" + e, 1, reads, writes, cost, cost))
 
-    def dma(e, sem, out, in_, reads, writes, lat=2.2):
+    def dma(e, sem, out, in_, reads, writes, lat=LAT, first=0.0):
+        bonus[len(tasks)] = first
         tasks.append((e, "dma", lambda q: q.dma_start(out, in_), sem, 16, reads, writes, 0.1, lat))
 
     def ap(rg):
@@ -61,17 +64,17 @@ def rank_program(g, core, T, topo):
         return all(SCRATCH[x[0]][0] == "sbuf" and SCRATCH[x[0]][2] in (BF, U2, F2) for x in rgs)
 
     def vc(n, f=1.0):
-        return 0.05 + max(64, n * f) * CY
+        return 0.02 + max(64, n * f) * CY
 
     def copy(e, out, in_):
         n = in_[2] - in_[1]
         if e == "v":
             op("v", lambda q: q.tensor_copy(ap(out), ap(in_)), [in_], [out], vc(n, 0.5 if small(out, in_) else 1))
         else:
-            op("a", lambda q: q.activation(ap(out), ap(in_), AF.Copy), [in_], [out], 0.15 + n * CY)
+            op("a", lambda q: q.activation(ap(out), ap(in_), AF.Copy), [in_], [out], 0.05 + n * CY)
 
     def act(out, in_, func):
-        op("a", lambda q: q.activation(ap(out), ap(in_), func), [in_], [out], 0.15 + (in_[2] - in_[1]) * CY)
+        op("a", lambda q: q.activation(ap(out), ap(in_), func), [in_], [out], 0.05 + (in_[2] - in_[1]) * CY)
 
     def tt(out, a, b, o):
         f = 1 if a[0].startswith("ps") or b[0].startswith("ps") else 2
@@ -112,9 +115,9 @@ def rank_program(g, core, T, topo):
 
     XW, AW, IW = full("xs"), full("adjs"), full("iot")
 
-    dma("s", "ltv", T.tvs[:, :], T.tv[:, :], [], [full("tvs")])
-    dma("s", "ladj", T.adjs[:, :], T.adj[:, :], [], [full("adjs")], 9.0)
-    dma("s", "lx", T.xs[:, 0:4096], T.x[:, :], [], [("xs", 0, 4096)], 13.0)
+    dma("s", "ltv", T.tvs[:, :], T.tv[:, :], [], [full("tvs")], LAT, 1000.0)
+    dma("s", "ladj", T.adjs[:, :], T.adj[:, :], [], [full("adjs")], 7.0, 500.0)
+    dma("s", "lx", T.xs[:, 0:4096], T.x[:, :], [], [("xs", 0, 4096)], 10.0, 400.0)
 
     def fill(rg, val, cost):
         op("v", lambda q: q.memset(ap(rg), val), [], [rg], cost)
@@ -128,25 +131,30 @@ def rank_program(g, core, T, topo):
         op("g", lambda q: q.affine_select(ap(out), ap(in_), pat, cmp, 0.0, base, cm), [in_], [out], 0.2 + 2 * CY * (in_[2] - in_[1]))
 
     one128 = full("ones")
-    op("g", lambda q: q.iota(T.iot[:, :], [[1, 4096]], 0, 0), [], [full("iot")], 8.2)
+    lift[0] = 300.0
     asel(full("c1"), ("ones", 0, 8), [[-16, 8]], OP.is_ge, 0, 1)
     asel(full("c2"), full("c1"), [[16, 8]], OP.is_ge, 15, -1)
     asel(full("im"), one128, [[-1, 128]], OP.is_equal, 0, 1)
     asel(full("b1"), one128, [[-16, 8], [0, 16]], OP.is_ge, 0, 1)
     asel(full("bm"), full("b1"), [[16, 8], [0, 16]], OP.is_ge, 15, -1)
     asel(full("lt"), full("bm"), [[1, 128]], OP.is_gt, 0, -1)
+    lift[0] = 200.0
+    op("g", lambda q: q.iota(T.iot[:, :], [[1, 4096]], 0, 0), [], [full("iot")], 7.0)
+    lift[0] = 0.0
     asel(full("bcb"), full("bcb"), [[-1, 16], [-16, 8], [0, 16]], OP.is_equal, 0, 1)
 
-    def zeros(s):
-        op("g", lambda q: q.iota(ap(hw(s)), [[0, 4096]], 0, 0, allow_small_or_imprecise_dtypes=True), [], [hw(s)], 8.2)
+    def zeros(s, *after):
+        op("g", lambda q: q.iota(ap(hw(s)), [[0, 4096]], 0, 0, allow_small_or_imprecise_dtypes=True), list(after), [hw(s)], 7.0)
 
-    for s in range(NR if r != 3 else 3):
+    for s in range(2):
         zeros(s)
 
     def diag(i):
         op("v", lambda q: q.tensor_copy(T.gall[:, 128 * i + i:128 * i + 128:16], T.c2[:, :]), [full("c2")], [gi(i)], 0.12)
 
+    lift[0] = 200.0
     copy("v", full("tvu"), full("tvs"))
+    lift[0] = 0.0
     for i in range(16):
         diag(i)
     for nm, f in (("hi", 0.5), ("nhi", -0.5), ("ni", -1.0), ("pi", 512.0), ("pn", -512.0)):
@@ -161,16 +169,17 @@ def rank_program(g, core, T, topo):
     def rows_y(t):
         gather("v", blk("cj", t), AW, tj(t))
         gather("v", blk("yj", t), IW, tj(t))
-        dma("s", "sli%d_4" % t, ap(li(t, t)), T.cj[t::16, 512 * t:512 * t + 512], [blk("cj", t)], [li(t, t)], 2.4)
-        dma("s", "stl%d" % t, ap(tl(t)), T.yj[0::16, 512 * t:512 * t + 512], [blk("yj", t)], [tl(t)])
+        dma("s", "sli%d_4" % t, ap(li(t, t)), T.cj[t::16, 512 * t:512 * t + 512], [blk("cj", t)], [li(t, t)], LAT, 50.0)
+        dma("s", "stl%d" % t, ap(tl(t)), T.yj[0::16, 512 * t:512 * t + 512], [blk("yj", t)], [tl(t)], LAT, 50.0)
         for n, i in enumerate([i for i in range(16) if i != t]):
             dma("s" if n % 2 or t else "a", "sli%d_%d" % (t, n // 4), ap(li(t, i)), T.cj[i::16, 512 * t:512 * t + 512],
-                [blk("cj", t)], [li(t, i)], 2.5 + 0.3 * n)
+                [blk("cj", t)], [li(t, i)], LAT + 0.12 * n)
 
-    for t in range(NR):
-        rows_v(t)
-    for t in range(NR):
-        rows_y(t)
+    for fn in (rows_v, rows_y):
+        for t in range(NR):
+            lift[0] = 60.0 - 10 * t
+            fn(t)
+    lift[0] = 0.0
 
     def prep(t):
         b = t % 2
@@ -179,19 +188,20 @@ def rank_program(g, core, T, topo):
         gather("a", xv, XW, li(t, t))
         mm(full("psX"), full("hi"), xv, True, False)
         mm(full("psX"), full("hi"), xy, False, True)
-        mm(full("psY"), full("hi"), xv, True, False)
-        mm(full("psY"), full("nhi"), xy, False, True)
         copy("a", blk("m", 2 * b), full("psX"))
         copy("a", blk("m", 2 * b + 1), full("psX"))
-        act(hb, full("psY"), AF.Abs)
+        mm(full("psX"), full("hi"), xv, True, False)
+        mm(full("psX"), full("nhi"), xy, False, True)
+        act(hb, full("psX"), AF.Abs)
 
     def mins(t):
+        n = NR if t == r else t + 1
         lk, yl, mn = blk("lki", t, 128), blk("yli", t, 32), blk("mini", t, 128)
         copy("v", lk, ("li", 512 * t, 512 * t + 128))
         copy("v", yl, tl(t))
-        for s in range(NR):
+        for s in range(n):
             tt(blk("mini", 4 * t + s, 32), blk("lki", 4 * t + s, 32), yl, OP.min)
-        copy("v", blk("mint", t, 128), mn)
+        copy("v", ("mint", 128 * t, 128 * t + 32 * n), ("mini", 128 * t, 128 * t + 32 * n))
 
     def cols(t):
         zc, inv, eq, off = blk("zc", t), blk("inv", t), blk("eq", t), tl(t)
@@ -216,11 +226,12 @@ def rank_program(g, core, T, topo):
         us = []
         k = 0
         while k < len(ent):
-            n = 2 if k + 1 < len(ent) and ent[k + 1] == ent[k] + 1 else 1
+            n = 2 if t < 3 and k + 1 < len(ent) and ent[k + 1] == ent[k] + 1 else 1
             us.append((t, ent[k], n))
             k += n
         for j, u in enumerate(us):
             units.append(u + (j == 0, j == len(us) - 1))
+    start = [n for n, u in enumerate(units) if u[3]] + [len(units)]
 
     def unit(n):
         t, i, k, fst, lst = units[n]
@@ -246,7 +257,7 @@ def rank_program(g, core, T, topo):
     def remote(name, t, transfers, nloc, nrem, src, land):
         tasks.append(("g", "send", lambda q: q.remote_dma_fused(transfers, local_sem=T.sem.loc), "loc", nloc, [src],
                       [("token" + name, t, t + 1)], 0.6, 0.6))
-        tasks.append((None, "land", None, name + str(t), 3 * nrem, [("token" + name, t, t + 1)], land, 0.0, 4.5))
+        tasks.append((None, "land", None, name + str(t), 3 * nrem, [("token" + name, t, t + 1)], land, 0.0, LAND[name]))
 
     def share(t):
         mine = blk("part", t)
@@ -265,14 +276,14 @@ def rank_program(g, core, T, topo):
     def mi(t, s):
         return blk("mint", 4 * t + s, 32)
 
-    def look(e, t, s):
+    def look(t, s):
         if t == r:
-            gather(e, rk(t, s), hw(s), mi(t, s))
+            gather("a", rk(t, s), hw(s), mi(t, s))
         else:
-            gather(e, part(rk(t, s), r), hw(s), part(mi(t, s), r))
+            gather("a", part(rk(t, s), r), hw(s), part(mi(t, s), r))
 
     def decide(t):
-        X, Y = ("psX", 0, 128), ("psY", 0, 128)
+        X = ("psY", 0, 128)
         mm(X, full("pi"), part(blk("eq", t), r), True, False)
         mm(X, full("pi"), part(blk("inv", t), r), False, False)
         for s in range(t):
@@ -285,10 +296,10 @@ def rank_program(g, core, T, topo):
         mm(X, full("qm"), full("ok"), True, True)
         ts(full("first"), X, -1.0, OP.is_equal)
         tt(full("fz"), full("first"), part(blk("zc", t), r), OP.mult)
-        mm(Y, full("b2k"), full("first"), True, False)
-        mm(Y, full("nbm"), full("fz"), False, True)
+        mm(X, full("b2k"), full("first"), True, False)
+        mm(X, full("nbm"), full("fz"), False, True)
         mine = part(blk("sepin", t), r)
-        copy("a", mine, Y)
+        copy("v", mine, X)
         tr = [RemoteDMATransfer(dst_ids=[dst(q) for q in others], dma_engine_mask=topo.mask(core, T.cores[others[0]]),
                                 remote_sem=T.sem["sar%d" % t], srcs=[ap(mine)], dsts=[ap(mine) for _ in others])]
         remote("sar", t, tr, len(links), len(links), mine, [part(blk("sepin", t), q) for q in others])
@@ -306,7 +317,7 @@ def rank_program(g, core, T, topo):
         dma("s", "osep%d" % t, T.ysep[:, a:b], T.sepf[0::16, a:b], [("sepf", a, b)], [])
 
     def half(a, b, src, out):
-        op("a", lambda q: q.activation(T.sepf[:, a:b:2], ap(src), AF.Identity, bias=4096.0, scale=-1.0), [src], [out], 0.4)
+        op("v", lambda q: q.tensor_scalar(T.sepf[:, a:b:2], ap(src), -1.0, 4096.0, OP.mult, OP.add), [src], [out], vc(256))
 
     def mj(j):
         return blk("mt_", j)
@@ -318,7 +329,7 @@ def rank_program(g, core, T, topo):
         for s in range(NR):
             dma("s", "slv", ap(blk("lv", s, 32)), T.cvj[s::16, :], [full("cvj")], [blk("lv", s, 32)])
         gather_less(full("cvl"), AW, li(r, r))
-        op("v", lambda q: q.tensor_scalar(T.w4[:, :], ap(blk("zc", r)), -1.0, 2048.0, OP.mult, OP.add), [blk("zc", r)], [full("w4")], vc(512))
+        ts(full("w4"), blk("zc", r), 2048.0, OP.add)
         copy("v", full("lvi"), full("lv"))
         copy("v", full("vli"), li(r, r))
         for s in range(NR):
@@ -335,42 +346,50 @@ def rank_program(g, core, T, topo):
         copy("a", full("base"), Z)
 
     def fl_own():
-        tt(full("eqs"), blk("sepin", r), full("w4"), OP.is_equal)
+        for n in range(2):
+            own_half(512 * r + n, 512 * r + 512, part(full("w4"), n, 2), part(full("eqs"), n, 2))
         ts(full("nh"), blk("sepin", r), 0.0, OP.is_equal)
 
-    def fl_round(e, s):
-        if s != r:
-            gather(e, blk("rv", s), hw(s), blk("mv", s, 32))
-            if s > r:
-                look(e, r, s)
-            tt(blk("mg", s), mj(s), blk("rv", s), OP.is_gt)
+    def own_half(a, b, w, out):
+        op("v", lambda q: q.tensor_tensor(ap(out), T.sepf[:, a:b:2], ap(w), OP.is_equal), [("sepf", a, b), w], [out], vc(256, 2))
 
-    prep(0)
-    bigmats()
-    cols(r)
-    per = len(units) // NR
+    def fl_round(s):
+        if s != r:
+            gather("v", blk("rv", s), hw(s), blk("mv", s, 32))
+            if s > r:
+                look(r, s)
+            mm(full("psZ"), full("im"), mj(s), True, True)
+            tt(blk("mg", s), full("psZ"), blk("rv", s), OP.is_gt)
+
     for t in range(NR):
-        if t:
-            prep(t)
+        lift[0] = 20.0 if t else 60.0
+        prep(t)
+        lift[0] = 0.0
+        if t == 0:
+            bigmats()
+            cols(r)
         mins(t)
         if t != r:
             cols(t)
-        for n in range(per):
-            unit(per * t + n)
+        for n in range(start[t + 1] - start[t]):
+            unit(start[t] + n)
             if t and n == 2:
                 for s in range(t - 1):
-                    look("v", t, s)
+                    look(t, s)
                 decide(t - 1)
             if t and n == 5:
                 mark(t - 1)
-                look("v", t, t - 1)
+                look(t, t - 1)
                 seps(t - 1)
                 if t - 1 == r:
                     fl_own()
-                fl_round("v", t - 1)
+                fl_round(t - 1)
         if t == 0:
             fl_static()
         share(t)
+        if t == 0:
+            for s in range(2, NR if r != 3 else 3):
+                zeros(s, ("tokenarr", 0, 1))
     F = full("psA")
     mm(F, full("im"), full("base"), True, False)
     for s in range(3):
@@ -383,14 +402,15 @@ def rank_program(g, core, T, topo):
     decide(3)
     mark(3)
     if r != 3:
-        fl_round("a", 3)
+        fl_round(3)
         mm(F, blk("gn", 3, 128), rk(r, 3), False, False)
         mm(F, full("im"), blk("mg", 3), False, True)
+        seps(3)
     else:
+        seps(3)
         fl_own()
         mm(F, full("pn"), full("nh"), False, False)
         mm(F, full("pn"), full("eqs"), False, True)
-    seps(3)
     op("v", lambda q: q.tensor_scalar(T.fl[:, 0::2], T.psA[:, 0:256], 0.0, None, OP.is_gt), [F], [full("fl")], 0.3)
     op("v", lambda q: q.tensor_scalar(T.fl[:, 1::2], T.psA[:, 256:512], 0.0, None, OP.is_gt), [F], [full("fl")], 0.3)
     dma("s", "oflag", T.yflag[:, :], T.fl[:, :], [full("fl")], [])
@@ -409,7 +429,7 @@ def rank_program(g, core, T, topo):
                 clock[e][k] = v
         clock[e][sem] = max(clock[e].get(sem, 0), val)
 
-    for x in schedule(tasks):
+    for x in schedule(tasks, bonus):
         e, kind, fn, sem, inc, reads, writes, _, _ = tasks[x]
         reads = [q for q in reads if not q[0].startswith("token")]
         writes = [q for q in writes if not q[0].startswith("token")]
@@ -458,7 +478,7 @@ def rank_program(g, core, T, topo):
             clock["g"][sem] = val
 
 
-def schedule(tasks):
+def schedule(tasks, bonus):
     n = len(tasks)
     deps = [set() for _ in range(n)]
     recs, group = {}, {}
@@ -488,6 +508,7 @@ def schedule(tasks):
     prio = [0.0] * n
     for x in range(n - 1, -1, -1):
         prio[x] = tasks[x][8] + WAKE + max([prio[y] for y in succ[x]], default=0.0)
+    prio = [prio[x] + bonus.get(x, 0.0) for x in range(n)]
     left = [len(deps[x]) for x in range(n)]
     at = [0.0] * n
     free = {}

@@ -6,29 +6,33 @@ ND = 4
 BF, U2, F4, F2, I4 = "bfloat16", "uint16", "float32", "float16", "int32"
 SCRATCH = {}
 for _n, _w, _d in (
-        ("adjs", 4096, I4), ("xs", 4112, BF), ("tvs", 128, I4), ("tvu", 128, U2), ("iot", 4096, I4), ("ones", 128, BF),
-        ("c1", 8, BF), ("c2", 8, BF), ("b1", 128, BF), ("bm", 128, BF), ("im", 128, BF), ("lt", 128, BF), ("q16", 128, BF),
-        ("qm", 128, BF), ("hi", 128, BF), ("nhi", 128, BF), ("ni", 128, BF), ("pi", 128, BF), ("pn", 128, BF),
-        ("nbm", 128, F2), ("b2k", 128, F2), ("bcb", 2048, BF), ("bch", 2048, F2), ("gall", 2048, BF), ("gp", 512, BF),
-        ("gn", 512, BF), ("ve", 512, U2), ("vj", 32, U2), ("cvj", 512, U2), ("lv", 128, U2), ("lvi", 128, I4), ("vli", 32, I4),
-        ("mvi", 128, I4), ("mv", 128, U2), ("cvl", 512, F2), ("w4", 512, F4), ("mt_", 8192, BF), ("base", 512, BF),
-        ("eqs", 512, BF), ("nh", 512, BF), ("fl", 512, BF), ("wsum", 128, BF), ("ok", 128, BF), ("first", 128, F2),
-        ("fz", 128, F2), ("tj", 128, U2), ("tl", 128, U2), ("mint", 512, U2), ("eq", 2048, BF), ("inv", 2048, BF),
-        ("lki", 512, I4), ("yli", 128, I4), ("mini", 512, I4), ("ce", 2048, U2), ("cj", 2048, U2), ("yj", 2048, U2),
-        ("li", 2048, U2), ("zc", 2048, F2), ("h", 16384, BF), ("part", 2048, BF), ("pin", 2048, BF), ("sepin", 2048, U2),
-        ("sepf", 2048, F4), ("rv", 2048, BF), ("mg", 2048, BF), ("rk", 8192, BF), ("xv", 1024, BF), ("xy", 1024, BF),
-        ("m", 2048, F4), ("hh", 1024, BF), ("d", 1024 * ND, BF), ("w", 3072, BF), ("s", 3072, BF)):
+        ("adjs", 4096, I4), ("xs", 4112, BF), ("tvs", 128, I4), ("tvu", 128, U2), ("ones", 128, BF),
+        ("c1", 8, BF), ("c2", 8, BF), ("b1", 128, BF), ("bm", 128, BF), ("im", 128, BF), ("lt", 128, BF),
+        ("ev", 128, BF), ("od", 128, BF), ("dp", 128, BF), ("dm", 128, BF), ("de", 128, BF), ("do", 128, BF),
+        ("s00", 128, F2), ("s01", 128, F2), ("s10", 128, F2), ("s11", 128, F2), ("ut", 512, F2), ("cjf", 512, F2),
+        ("q16", 128, BF), ("qm", 128, BF), ("hi", 128, BF), ("nhi", 128, BF), ("ni", 128, BF), ("pi", 128, BF), ("pn", 128, BF),
+        ("imf", 128, F2), ("nif", 128, F2), ("nbm", 128, F2), ("b2k", 128, F2), ("bcb", 2048, BF), ("bch", 2048, F2),
+        ("gall", 2048, BF), ("gp", 512, BF), ("gn", 512, BF), ("zj", 128, F2), ("zz", 128, F2), ("tlf", 128, F2),
+        ("zv", 32, F2), ("vj", 32, U2), ("cvj", 512, U2), ("lv", 128, U2), ("lvi", 128, I4), ("mvi", 128, I4), ("mv", 128, U2),
+        ("sf", 512, F2), ("mt_", 8192, BF), ("eqs", 512, BF), ("nh", 512, BF), ("fl", 512, BF), ("wsum", 256, BF),
+        ("ok", 256, BF), ("first", 256, F2), ("fz", 256, F2), ("tj", 128, U2), ("tl", 128, U2), ("mint", 512, U2),
+        ("eq", 2048, BF), ("inv", 2048, BF), ("lki", 512, I4), ("yli", 128, I4), ("mini", 512, I4), ("ce", 2048, F2),
+        ("cj", 2048, U2), ("li", 2048, U2), ("zc", 2048, F2), ("h", 16384, BF), ("part", 2048, BF), ("pin", 3584, BF),
+        ("sepin", 2048, U2), ("sepf", 2048, F4), ("rv", 2048, BF), ("mg", 2048, BF), ("rk", 8192, BF), ("xv", 1024, BF),
+        ("xy", 1024, BF), ("m", 2048, F4), ("hh", 1024, BF), ("d", 1024 * ND, BF), ("w", 3072, BF), ("s", 3072, BF)):
     SCRATCH[_n] = ("sbuf", [128, _w], _d)
-for _n, _w in (("psT", 2048), ("psA", 512), ("psX", 512), ("psY", 512), ("psZ", 512)):
+for _n, _w in (("psT", 2048), ("psA", 512), ("psX", 512), ("psW", 1024)):
     SCRATCH[_n] = ("psum", [128, _w], F4)
 
-SEMAPHORES = ["cv", "ca", "cp", "cg", "ltv", "ladj", "lx", "loc", "svj", "slv", "oflag"]
+SEMAPHORES = ["cv", "ca", "cp", "cg", "ltv", "ladj", "lx", "loc", "svj", "slv", "oflag", "brr3"]
 for _t in range(NR):
-    SEMAPHORES += ["%s%d" % (_k, _t) for _k in ("arr", "sar", "stj", "stl", "osep")] + ["sli%d_%d" % (_t, _k) for _k in range(5)]
+    SEMAPHORES += ["%s%d" % (_k, _t) for _k in ("arr", "sar", "stj", "stl", "mdp", "osep")]
+    SEMAPHORES += ["sli%d_%d" % (_t, _k) for _k in range(8)]
 
-CY, GA, SC, PE = 0.9e-3, 1.55, 3.6, 0.43e-3
+CY, GA, SC, PE = 0.9e-3, 1.5, 2.8, 0.43e-3
 WAKE, LAT = 0.05, 2.2
-LAND = {"arr": 4.0, "sar": 6.5}
+LATE = 20.0
+LAND = {"arr": 3.0, "sar": 4.0, "brr": 4.0}
 
 
 def rank_program(g, core, T, topo):
@@ -95,8 +99,8 @@ def rank_program(g, core, T, topo):
     def gather_less(out, win, off):
         op("v", lambda q: q.tensor_scalar(ap(out), ap(win).indirect(ap(off)), -2048.0, None, OP.add), [win, off], [out], gcost(off))
 
-    def mm(out, lhs, rhs, start, stop):
-        op("p", lambda q: q.matmul(ap(out), ap(lhs), ap(rhs), start, stop), [lhs, rhs], [out], 0.03 + (rhs[2] - rhs[1]) * PE)
+    def mm(out, lhs, rhs, start, stop, bank=None):
+        op("p", lambda q: q.matmul(ap(out), ap(lhs), ap(rhs), start, stop), [lhs, rhs], [bank or out], 0.03 + (rhs[2] - rhs[1]) * PE)
 
     def gi(i):
         return blk("gall", i, 128)
@@ -110,10 +114,16 @@ def rank_program(g, core, T, topo):
     def li(t, i, n=1):
         return ("li", 512 * t + 32 * i, 512 * t + 32 * i + 32 * n)
 
+    def li3(n, i, k=1):
+        return ("li", 1536 + 256 * n + 16 * i, 1536 + 256 * n + 16 * i + 16 * k)
+
     def hw(t):
         return blk("h", t, 4096)
 
-    XW, AW, IW = full("xs"), full("adjs"), full("iot")
+    def psz(w=512):
+        return ("psW", 512, 512 + w)
+
+    XW, AW = full("xs"), full("adjs")
 
     dma("s", "ltv", T.tvs[:, :], T.tv[:, :], [], [full("tvs")], LAT, 1000.0)
     dma("s", "ladj", T.adjs[:, :], T.adj[:, :], [], [full("adjs")], 7.0, 500.0)
@@ -122,7 +132,9 @@ def rank_program(g, core, T, topo):
     def fill(rg, val, cost):
         op("v", lambda q: q.memset(ap(rg), val), [], [rg], cost)
 
+    lift[0] = 200.0
     fill(full("ones"), 1.0, 0.1)
+    lift[0] = 0.0
     fill(full("bcb"), 1.0, 1.0)
     fill(full("gall"), 0.0, 1.0)
     fill(("xs", 4096, 4112), 0.0, 0.1)
@@ -135,11 +147,17 @@ def rank_program(g, core, T, topo):
     asel(full("c1"), ("ones", 0, 8), [[-16, 8]], OP.is_ge, 0, 1)
     asel(full("c2"), full("c1"), [[16, 8]], OP.is_ge, 15, -1)
     asel(full("im"), one128, [[-1, 128]], OP.is_equal, 0, 1)
+    half = [[0, 4], [-1, 2], [0, 16]]
+    asel(full("ev"), full("im"), half, OP.is_equal, 0, 0)
+    asel(full("od"), full("im"), half, OP.is_equal, 1, 0)
+    asel(full("dp"), one128, [[-1, 128]], OP.is_equal, -16, 1)
+    asel(full("dm"), one128, [[-1, 128]], OP.is_equal, 16, 1)
+    asel(full("de"), full("dp"), half, OP.is_equal, 0, 0)
+    asel(full("do"), full("dm"), half, OP.is_equal, 1, 0)
+    lift[0] = 250.0
     asel(full("b1"), one128, [[-16, 8], [0, 16]], OP.is_ge, 0, 1)
     asel(full("bm"), full("b1"), [[16, 8], [0, 16]], OP.is_ge, 15, -1)
     asel(full("lt"), full("bm"), [[1, 128]], OP.is_gt, 0, -1)
-    lift[0] = 200.0
-    op("g", lambda q: q.iota(T.iot[:, :], [[1, 4096]], 0, 0), [], [full("iot")], 7.0)
     lift[0] = 0.0
     asel(full("bcb"), full("bcb"), [[-1, 16], [-16, 8], [0, 16]], OP.is_equal, 0, 1)
 
@@ -147,71 +165,157 @@ def rank_program(g, core, T, topo):
         op("g", lambda q: q.iota(ap(hw(s)), [[0, 4096]], 0, 0, allow_small_or_imprecise_dtypes=True), list(after), [hw(s)], 7.0)
 
     for s in range(2):
-        zeros(s)
+        zeros(s, full("lt"))
 
     def diag(i):
         op("v", lambda q: q.tensor_copy(T.gall[:, 128 * i + i:128 * i + 128:16], T.c2[:, :]), [full("c2")], [gi(i)], 0.12)
 
     lift[0] = 200.0
     copy("v", full("tvu"), full("tvs"))
+    for a, b in (("s00", "ev"), ("s11", "od"), ("s10", "de"), ("s01", "do")):
+        copy("v", full(a), full(b))
     lift[0] = 0.0
     for i in range(16):
         diag(i)
-    for nm, f in (("hi", 0.5), ("nhi", -0.5), ("ni", -1.0), ("pi", 512.0), ("pn", -512.0)):
+    for nm, f in (("hi", 0.5), ("nhi", -0.5), ("ni", -1.0), ("pi", 512.0), ("pn", -512.0), ("imf", 1.0), ("nif", -1.0)):
         ts(full(nm), full("im"), f, OP.mult)
     ts(full("gp"), ("gall", 0, 512), 64.0, OP.mult)
     ts(full("gn"), ("gall", 0, 512), -64.0, OP.mult)
 
+    SEL = [["s00", "s01"], ["s10", "s11"]]
+
+    def flip(rows):
+        op("v", lambda q: q.transpose(T.ut[:, :], ap(rows)), [rows], [full("ut")], vc(256))
+
+    def pick(u, h):
+        op("p", lambda q: q.matmul(T.psX[:, 16 * u:16 * u + 16], T[SEL[u][h]][:, :], T.ut[:, 16 * h:512:32], h == 0, h == 1),
+           [full(SEL[u][h]), full("ut")], [("psX", 0, 32)], 0.06)
+
+    def ylist(u):
+        op("v", lambda q: q.tensor_scalar(T.tl[:, u:32:2], T.psX[:, 16 * u:16 * u + 16], 2048.0, None, OP.add),
+           [("psX", 0, 32)], [tl(0)], vc(16))
+
+    def ymix(u):
+        op("v", lambda q: q.tensor_copy(T.tj[:, u:32:2], T.tl[:, 16 * u:16 * u + 16]), [tl(0)], [tj(0)], vc(16))
+
+    def entry(i):
+        op("v", lambda q: q.tensor_scalar(ap(li(0, i)), T.psW[:, i:1024:32], 2048.0, None, OP.add), [full("psW")], [li(0, i)], vc(32))
+
+    def first_lists():
+        gather_less(blk("ce", 0), AW, blk("tvu", 0, 32))
+        flip(blk("ce", 0))
+        for u in range(2):
+            for h in range(2):
+                pick(u, h)
+        for u in range(2):
+            ylist(u)
+        for u in range(2):
+            ymix(u)
+        gather_less(full("cjf"), AW, tj(0))
+        flip(full("cjf"))
+        for u in range(2):
+            for h in range(2):
+                mm(("psW", 512 * u, 512 * u + 496), full(SEL[u][h]), ("ut", 16 * h, 16 * h + 496), h == 0, h == 1)
+        for i in range(1, 16):
+            entry(i)
+
     def rows_v(t):
-        gather("v", blk("ce", t), AW, blk("tvu", t, 32))
-        dma("s", "stj%d" % t, ap(tj(t)), T.ce[t::16, 512 * t:512 * t + 512], [blk("ce", t)], [tj(t)])
+        a, b = 512 * t, 32 * t
+        gather_less(blk("ce", t), AW, blk("tvu", t, 32))
+        for n in range(2):
+            dma("s", "stj%d" % t, T.zj[:, b + 16 * n:b + 16 * n + 16], T.ce[t::16, a + 256 * n:a + 256 * n + 256],
+                [blk("ce", t)], [("zj", b + 16 * n, b + 16 * n + 16)], LAT, 50.0)
+        for n in range(2):
+            dma("s", "stl%d" % t, T.zz[:, b + 16 * n:b + 16 * n + 16], T.ce[t + 16 * n::32, a:a + 512],
+                [blk("ce", t)], [("zz", b + 16 * n, b + 16 * n + 16)], LAT, 40.0)
+
+    def plus(out, a, b, step, src):
+        op("v", lambda q: q.tensor_scalar(T[out][:, a:b:step], ap(src), 2048.0, None, OP.add), [src], [(out, a, b)], vc(16))
 
     def rows_y(t):
+        b = 32 * t
+        if t == 3:
+            plus("tj", b, b + 32, 1, ("zj", b, b + 32))
+        else:
+            for n in range(2):
+                plus("tj", b + n, b + 32, 2, ("zj", b + 16 * n, b + 16 * n + 16))
         gather("v", blk("cj", t), AW, tj(t))
-        gather("v", blk("yj", t), IW, tj(t))
-        dma("s", "sli%d_4" % t, ap(li(t, t)), T.cj[t::16, 512 * t:512 * t + 512], [blk("cj", t)], [li(t, t)], LAT, 50.0)
-        dma("s", "stl%d" % t, ap(tl(t)), T.yj[0::16, 512 * t:512 * t + 512], [blk("yj", t)], [tl(t)], LAT, 50.0)
-        for n, i in enumerate([i for i in range(16) if i != t]):
-            dma("s" if n % 2 or t else "a", "sli%d_%d" % (t, n // 4), ap(li(t, i)), T.cj[i::16, 512 * t:512 * t + 512],
+        op("v", lambda q: q.transpose(T.tlf[:, b:b + 32], T.zz[:, b:b + 32]), [("zz", b, b + 32)], [("tlf", b, b + 32)], vc(32))
+        plus("tl", b, b + 32, 1, ("tlf", b, b + 32))
+        rest = [i for i in range(16) if i != t]
+        if t == 3:
+            for n in range(2):
+                for k, i in enumerate(rest):
+                    z = li3(n, i)
+                    dma("s", "sli3_%d" % ((15 * n + k) // 4), ap(z), T.cj[i::16, 1536 + 256 * n:1792 + 256 * n], [blk("cj", t)], [z],
+                        LAT + 0.12 * k)
+            return
+        for n, i in enumerate(rest):
+            dma("s", "sli%d_%d" % (t, n // 4), ap(li(t, i)), T.cj[i::16, 512 * t:512 * t + 512],
                 [blk("cj", t)], [li(t, i)], LAT + 0.12 * n)
 
+    lift[0] = 60.0
+    first_lists()
     for fn in (rows_v, rows_y):
-        for t in range(NR):
-            lift[0] = 60.0 - 10 * t
+        for t in range(1, NR):
+            lift[0] = 60.0 - 5 * t
             fn(t)
     lift[0] = 0.0
 
     def prep(t):
         b = t % 2
         xv, xy, hb = blk("xv", b), blk("xy", b), blk("hh", b)
+        gather("a", xv, XW, blk("tvu", t, 32))
         gather("a", xy, XW, tl(t))
-        gather("a", xv, XW, li(t, t))
         mm(full("psX"), full("hi"), xv, True, False)
         mm(full("psX"), full("hi"), xy, False, True)
-        copy("a", blk("m", 2 * b), full("psX"))
-        copy("a", blk("m", 2 * b + 1), full("psX"))
+        if t == 3:
+            for n in range(2):
+                m1, m2 = ("m", 1024 + 512 * n, 1280 + 512 * n), ("m", 1280 + 512 * n, 1536 + 512 * n)
+                copy("a", m1, ("psX", 256 * n, 256 * n + 256))
+                dma("s", "mdp3", ap(m2), ap(m1), [m1], [m2], LAT + 0.3)
+        else:
+            m1, m2 = blk("m", 2 * b), blk("m", 2 * b + 1)
+            copy("a", m1, full("psX"))
+            if t:
+                dma("s", "mdp%d" % t, ap(m2), ap(m1), [m1], [m2], LAT + 0.6)
+            else:
+                copy("a", m2, full("psX"))
         mm(full("psX"), full("hi"), xv, True, False)
         mm(full("psX"), full("nhi"), xy, False, True)
         act(hb, full("psX"), AF.Abs)
 
     def mins(t):
         n = NR if t == r else t + 1
-        lk, yl, mn = blk("lki", t, 128), blk("yli", t, 32), blk("mini", t, 128)
-        copy("v", lk, ("li", 512 * t, 512 * t + 128))
+        yl = blk("yli", t, 32)
         copy("v", yl, tl(t))
-        for s in range(n):
-            tt(blk("mini", 4 * t + s, 32), blk("lki", 4 * t + s, 32), yl, OP.min)
+        tt(blk("mini", 5 * t, 32), blk("tvs", t, 32), yl, OP.min)
+        if t == 3:
+            for k in range(2):
+                b = 384 + 64 * k
+                copy("v", ("lki", b, b + 48), li3(k, 0, 3))
+                for s in range(3):
+                    tt(part(blk("mini", 12 + s, 32), k, 2), ("lki", b + 16 * s, b + 16 * s + 16), part(yl, k, 2), OP.min)
+        else:
+            for a, b in ((0, t), (t + 1, n)):
+                if a < b:
+                    copy("v", ("lki", 128 * t + 32 * a, 128 * t + 32 * b), li(t, a, b - a))
+                for s in range(a, b):
+                    tt(blk("mini", 4 * t + s, 32), blk("lki", 4 * t + s, 32), yl, OP.min)
         copy("v", ("mint", 128 * t, 128 * t + 32 * n), ("mini", 128 * t, 128 * t + 32 * n))
 
     def cols(t):
         zc, inv, eq, off = blk("zc", t), blk("inv", t), blk("eq", t), tl(t)
-        if t != r:
+        if t not in (r, 3):
             zc, inv, off = part(zc, r), part(inv, r), part(off, r)
         gather_less(zc, AW, off)
         ts(inv, zc, 2048.0, OP.is_equal)
-        zq = part(blk("zc", t), r)
-        mm(("psZ", 0, 128), blk("bch", t, 128), zq, True, True)
-        tt(part(eq, r), ("psZ", 0, 128), zq, OP.is_equal)
+        zq = blk("zc", t)
+        if t < 3:
+            zq, eq = part(zq, r), part(eq, r)
+        z = psz(zq[2] - zq[1])
+        mm(z, blk("bch", t, 128), zq, True, True)
+        tt(eq, z, zq, OP.is_equal)
 
     def bigmats():
         copy("v", full("bch"), full("bcb"))
@@ -223,29 +327,37 @@ def rank_program(g, core, T, topo):
     units = []
     for t in range(NR):
         ent = [i for i in range(16) if i != t]
-        us = []
-        k = 0
-        while k < len(ent):
-            n = 2 if t < 3 and k + 1 < len(ent) and ent[k + 1] == ent[k] + 1 else 1
-            us.append((t, ent[k], n))
-            k += n
-        for j, u in enumerate(us):
-            units.append(u + (j == 0, j == len(us) - 1))
-    start = [n for n, u in enumerate(units) if u[3]] + [len(units)]
+        for c in range(2 if t == 3 else 1):
+            us = []
+            k = 0
+            while k < len(ent):
+                n = 2 if (t or k) and k + 1 < len(ent) and ent[k + 1] == ent[k] + 1 else 1
+                us.append((t, c, ent[k], n))
+                k += n
+            for j, u in enumerate(us):
+                units.append(u + (j == 0, j == len(us) - 1))
+    start = [[n for n, u in enumerate(units) if u[0] == t][0] for t in range(NR)] + [len(units)]
 
     def unit(n):
-        t, i, k, fst, lst = units[n]
-        c, d0, w0, p0, m0 = 512 * k, 1024 * (n % ND), 1024 * (n % 3), 1024 * (n % 2), 1024 * (t % 2)
+        t, ch, i, k, fst, lst = units[n]
+        wd = 256 if t == 3 else 512
+        c, d0, w0, p0, m0 = wd * k, 1024 * (n % ND), 1024 * (n % 3), 1024 * (n % 2), 1024 * (t % 2) + 512 * ch
         d, w, s, m, off = ("d", d0, d0 + c), ("w", w0, w0 + c), ("s", w0, w0 + c), ("m", m0, m0 + c), li(t, i, k)
+        hq, acc = blk("hh", t % 2), full("psA")
+        if t == 3:
+            off = li3(ch, i, k)
+            hq = part(hq, ch, 2)
+            acc = ("psX" if ch else "psA", 0, 256)
         op("v", lambda q: q.tensor_tensor(ap(d), ap(XW).indirect(ap(off)), ap(m), OP.subtract), [XW, off, m], [d], gcost(off))
         act(w, d, AF.Abs)
         for j in range(k):
-            o = ("psT", p0 + 512 * j, p0 + 512 * j + 512)
-            mm(o, full("im"), ("w", w0 + 512 * j, w0 + 512 * j + 512), True, False)
-            mm(o, full("ni"), blk("hh", t % 2), False, True)
+            o = ("psT", p0 + wd * j, p0 + wd * j + wd)
+            bank = ("psT", p0, p0 + 512) if t == 3 else o
+            mm(o, full("im"), ("w", w0 + wd * j, w0 + wd * j + wd), True, False, bank)
+            mm(o, full("ni"), hq, False, True, bank)
         act(s, ("psT", p0, p0 + c), AF.Sign)
         for j in range(k):
-            mm(full("psA"), gi(i + j), ("s", w0 + 512 * j, w0 + 512 * j + 512), fst and j == 0, lst and j == k - 1)
+            mm(acc, gi(i + j), ("s", w0 + wd * j, w0 + wd * j + wd), fst and j == 0, lst and j == k - 1)
 
     others = [q for q in range(NR) if q != r]
     links = topo.engines(core, T.cores[others[0]])
@@ -270,6 +382,18 @@ def rank_program(g, core, T, topo):
                                         srcs=[ap(part(mine, q))], dsts=[ap(part(blk("pin", t), r))]))
         remote("arr", t, tr, 3 * k, k, mine, [part(blk("pin", t), q) for q in others])
 
+    def pin3(q, a, b):
+        return ("pin", 1536 + 512 * q + a, 1536 + 512 * q + b)
+
+    def share_all(ch):
+        a = 256 * ch
+        mine = ("part", 1536 + a, 1792 + a)
+        copy("a", mine, ("psX" if ch else "psA", 0, 256))
+        name = "brr" if ch else "arr"
+        tr = [RemoteDMATransfer(dst_ids=[dst(q) for q in others], dma_engine_mask=topo.mask(core, T.cores[others[0]]),
+                                remote_sem=T.sem[name + "3"], srcs=[ap(mine)], dsts=[ap(pin3(r, a, a + 256)) for _ in others])]
+        remote(name, 3, tr, len(links), len(links), mine, [pin3(q, a, a + 256) for q in others])
+
     def rk(t, s):
         return blk("rk", 4 * t + s)
 
@@ -277,90 +401,102 @@ def rank_program(g, core, T, topo):
         return blk("mint", 4 * t + s, 32)
 
     def look(t, s):
-        if t == r:
+        if t in (r, 3):
             gather("a", rk(t, s), hw(s), mi(t, s))
         else:
             gather("a", part(rk(t, s), r), hw(s), part(mi(t, s), r))
 
-    def decide(t):
-        X = ("psY", 0, 128)
-        mm(X, full("pi"), part(blk("eq", t), r), True, False)
-        mm(X, full("pi"), part(blk("inv", t), r), False, False)
+    def decide(t, a, b):
+        def cut(rg):
+            return (rg[0], rg[1] + a, rg[1] + b)
+        w = b - a
+        X, W, K, FI, FZ = [(nm, 0, w) for nm in ("psW", "wsum", "ok", "first", "fz")]
+        mm(X, full("pi"), cut(blk("eq", t)), True, False)
+        mm(X, full("pi"), cut(blk("inv", t)), False, False)
         for s in range(t):
-            mm(X, blk("gp", s, 128), part(rk(t, s), r), False, False)
-        mm(X, full("im"), part(blk("part", t), r), False, False)
+            mm(X, blk("gp", s, 128), cut(rk(t, s)), False, False)
+        mm(X, full("im"), cut(blk("part", t)), False, False)
         for q in others:
-            mm(X, full("im"), part(blk("pin", t), q), False, q == others[-1])
-        act(full("wsum"), X, AF.Abs)
-        ts(full("ok"), full("wsum"), 8.0, OP.is_le)
-        mm(X, full("qm"), full("ok"), True, True)
-        ts(full("first"), X, -1.0, OP.is_equal)
-        tt(full("fz"), full("first"), part(blk("zc", t), r), OP.mult)
-        mm(X, full("b2k"), full("first"), True, False)
-        mm(X, full("nbm"), full("fz"), False, True)
-        mine = part(blk("sepin", t), r)
+            mm(X, full("im"), pin3(q, a, b) if t == 3 else part(blk("pin", t), q), False, q == others[-1])
+        act(W, X, AF.Abs)
+        ts(K, W, 8.0, OP.is_le)
+        mm(X, full("qm"), K, True, True)
+        ts(FI, X, -1.0, OP.is_equal)
+        tt(FZ, FI, cut(blk("zc", t)), OP.mult)
+        mm(X, full("b2k"), FI, True, False)
+        mm(X, full("nbm"), FZ, False, True)
+        mine = cut(blk("sepin", t))
         copy("v", mine, X)
+        if t == 3:
+            return
         tr = [RemoteDMATransfer(dst_ids=[dst(q) for q in others], dma_engine_mask=topo.mask(core, T.cores[others[0]]),
                                 remote_sem=T.sem["sar%d" % t], srcs=[ap(mine)], dsts=[ap(mine) for _ in others])]
         remote("sar", t, tr, len(links), len(links), mine, [part(blk("sepin", t), q) for q in others])
 
-    def mark(t):
+    def mark(t, a, b):
         if t == 3 and r == 3:
             return
-        off, src = mi(t, t), blk("sepin", t)
-        op("v", lambda q: q.tensor_copy(ap(hw(t)).indirect(ap(off)), ap(src)), [off, src], [hw(t)], 0.07 + 512 * SC * CY)
+        off, src = ("mint", 160 * t + a // 16, 160 * t + b // 16), ("sepin", 512 * t + a, 512 * t + b)
+        op("v", lambda q: q.tensor_copy(ap(hw(t)).indirect(ap(off)), ap(src)), [off, src], [hw(t)], 0.07 + (b - a) * SC * CY)
 
-    def seps(t):
-        a, b = 512 * t, 512 * t + 512
-        for n in range(2):
-            half(a + n, b, part(blk("sepin", t), n, 2), ("sepf", a, b))
-        dma("s", "osep%d" % t, T.ysep[:, a:b], T.sepf[0::16, a:b], [("sepf", a, b)], [])
-
-    def half(a, b, src, out):
-        op("v", lambda q: q.tensor_scalar(T.sepf[:, a:b:2], ap(src), -1.0, 4096.0, OP.mult, OP.add), [src], [out], vc(256))
+    def seps(t, a, b):
+        a, b = 512 * t + a, 512 * t + b
+        out, src = ("sepf", a, b), ("sepin", a, b)
+        op("v", lambda q: q.tensor_scalar(ap(out), ap(src), -1.0, 4096.0, OP.mult, OP.add), [src], [out], vc(b - a))
+        dma("s", "osep%d" % t, T.ysep[:, a:b], T.sepf[0::16, a:b], [out], [])
 
     def mj(j):
         return blk("mt_", j)
 
-    def fl_static():
-        gather("v", full("ve"), IW, blk("tvu", r, 32))
-        dma("s", "svj", T.vj[:, :], T.ve[0::16, :], [full("ve")], [full("vj")])
+    def fl_lists():
+        for n in range(2):
+            dma("s", "svj", T.zv[:, 16 * n:16 * n + 16], T.zc[r::16, 512 * r + 256 * n:512 * r + 256 * n + 256],
+                [blk("zc", r)], [("zv", 16 * n, 16 * n + 16)])
+        for n in range(2):
+            plus("vj", n, 32, 2, ("zv", 16 * n, 16 * n + 16))
         gather("v", full("cvj"), AW, full("vj"))
         for s in range(NR):
             dma("s", "slv", ap(blk("lv", s, 32)), T.cvj[s::16, :], [full("cvj")], [blk("lv", s, 32)])
-        gather_less(full("cvl"), AW, li(r, r))
-        ts(full("w4"), blk("zc", r), 2048.0, OP.add)
         copy("v", full("lvi"), full("lv"))
-        copy("v", full("vli"), li(r, r))
         for s in range(NR):
-            tt(blk("mvi", s, 32), blk("lvi", s, 32), full("vli"), OP.min)
-        copy("v", full("mv"), full("mvi"))
-        for j in range(16):
-            if j != r:
-                mm(full("psZ"), blk("bch", j, 128), full("cvl"), True, True)
-                tt(mj(j), full("psZ"), blk("zc", r), OP.is_equal)
-        Z = full("psZ")
-        mm(Z, full("pn"), blk("inv", r), True, False)
-        for j in range(4, 16):
-            mm(Z, full("im"), mj(j), False, j == 15)
-        copy("a", full("base"), Z)
+            if s != r:
+                tt(blk("mvi", s, 32), blk("lvi", s, 32), blk("tvs", r, 32), OP.min)
+        for a, b in ((0, r), (r + 1, NR)):
+            if a < b:
+                copy("v", ("mv", 32 * a, 32 * b), ("mvi", 32 * a, 32 * b))
 
-    def fl_own():
-        for n in range(2):
-            own_half(512 * r + n, 512 * r + 512, part(full("w4"), n, 2), part(full("eqs"), n, 2))
-        ts(full("nh"), blk("sepin", r), 0.0, OP.is_equal)
+    def match(j):
+        mm(psz(), blk("bch", j, 128), blk("ce", r), True, True)
+        tt(mj(j), psz(), blk("zc", r), OP.is_equal)
 
-    def own_half(a, b, w, out):
-        op("v", lambda q: q.tensor_tensor(ap(out), T.sepf[:, a:b:2], ap(w), OP.is_equal), [("sepf", a, b), w], [out], vc(256, 2))
+    def fl_own(a, b):
+        src, sf, z = ("sepin", 512 * r + a, 512 * r + b), ("sf", a, b), psz(b - a)
+        op("v", lambda q: q.tensor_scalar(ap(sf), ap(src), -1.0, 2048.0, OP.mult, OP.add), [src], [sf], vc((b - a) / 2))
+        mm(z, full("imf"), sf, True, False)
+        mm(z, full("nif"), ("zc", 512 * r + a, 512 * r + b), False, True)
+        ts(("eqs", a, b), z, 0.0, OP.is_equal)
+        ts(("nh", a, b), src, 0.0, OP.is_equal)
 
-    def fl_round(s):
+    def fl_gather(s):
         if s != r:
             gather("v", blk("rv", s), hw(s), blk("mv", s, 32))
             if s > r:
                 look(r, s)
-            mm(full("psZ"), full("im"), mj(s), True, True)
-            tt(blk("mg", s), full("psZ"), blk("rv", s), OP.is_gt)
 
+    def fl_round(s):
+        if s != r:
+            mm(psz(), full("im"), mj(s), True, s == 3)
+            if s == 3:
+                tt(blk("mg", s), psz(), blk("rv", s), OP.is_gt)
+            else:
+                mm(psz(), full("ni"), blk("rv", s), False, True)
+                act(blk("mg", s), psz(), AF.Relu)
+            mm(F, full("im"), blk("mg", s), False, s == 3)
+            if s != 3:
+                mm(F, blk("gn", s, 128), rk(r, s), False, False)
+
+    F = full("psA")
+    mine = (128 * r, 128 * r + 128)
     for t in range(NR):
         lift[0] = 20.0 if t else 60.0
         prep(t)
@@ -368,51 +504,60 @@ def rank_program(g, core, T, topo):
         if t == 0:
             bigmats()
             cols(r)
-        mins(t)
-        if t != r:
-            cols(t)
+            for k in range(NR):
+                mins(k)
+                if k != r:
+                    cols(k)
         for n in range(start[t + 1] - start[t]):
             unit(start[t] + n)
             if t and n == 2:
                 for s in range(t - 1):
                     look(t, s)
-                decide(t - 1)
+                decide(t - 1, *mine)
             if t and n == 5:
-                mark(t - 1)
+                mark(t - 1, 0, 512)
                 look(t, t - 1)
-                seps(t - 1)
-                if t - 1 == r:
-                    fl_own()
-                fl_round(t - 1)
+                seps(t - 1, 0, 512)
+                fl_gather(t - 1)
+            if units[start[t] + n][5] and t == 3:
+                share_all(units[start[t] + n][1])
         if t == 0:
-            fl_static()
-        share(t)
+            fl_lists()
+            lift[0] = LATE
+            for j in range(16):
+                if j != r:
+                    match(j)
+            lift[0] = 0.0
+        if t < 3:
+            share(t)
         if t == 0:
             for s in range(2, NR if r != 3 else 3):
                 zeros(s, ("tokenarr", 0, 1))
-    F = full("psA")
-    mm(F, full("im"), full("base"), True, False)
+    mm(F, full("pn"), blk("inv", r), True, False)
+    for j in range(4, 16):
+        mm(F, full("im"), mj(j), False, False)
     for s in range(3):
         if s != r:
-            mm(F, full("im"), blk("mg", s), False, False)
-            mm(F, blk("gn", s, 128), rk(r, s), False, False)
+            fl_round(s)
     if r != 3:
+        fl_own(0, 512)
         mm(F, full("pn"), full("eqs"), False, False)
         mm(F, full("pn"), full("nh"), False, False)
-    decide(3)
-    mark(3)
+    for c in range(2):
+        a, b = 256 * c, 256 * c + 256
+        decide(3, a, b)
+        mark(3, a, b)
+        seps(3, a, b)
+        if r == 3:
+            fl_own(a, b)
     if r != 3:
-        fl_round(3)
+        fl_gather(3)
         mm(F, blk("gn", 3, 128), rk(r, 3), False, False)
-        mm(F, full("im"), blk("mg", 3), False, True)
-        seps(3)
+        fl_round(3)
     else:
-        seps(3)
-        fl_own()
         mm(F, full("pn"), full("nh"), False, False)
         mm(F, full("pn"), full("eqs"), False, True)
-    op("v", lambda q: q.tensor_scalar(T.fl[:, 0::2], T.psA[:, 0:256], 0.0, None, OP.is_gt), [F], [full("fl")], 0.3)
-    op("v", lambda q: q.tensor_scalar(T.fl[:, 1::2], T.psA[:, 256:512], 0.0, None, OP.is_gt), [F], [full("fl")], 0.3)
+    ts(full("fl"), F, 0.0, OP.is_gt)
     dma("s", "oflag", T.yflag[:, :], T.fl[:, :], [full("fl")], [])
 
     cnt, snap, recs = {}, {}, {}

from concourse.bass import DstId, RemoteDMATransfer
from concourse.mybir import AluOpType as OP, ActivationFunctionType as AF

NR, E = 4, 512
ND = 4
BF, U2, F4, F2, I4 = "bfloat16", "uint16", "float32", "float16", "int32"
SCRATCH = {}
for _n, _w, _d in (
        ("adjs", 4096, I4), ("xs", 4112, BF), ("tvs", 128, I4), ("tvu", 128, U2), ("ones", 128, BF),
        ("c1", 8, BF), ("c2", 8, BF), ("b1", 128, BF), ("bm", 128, BF), ("im", 128, BF), ("lt", 128, BF),
        ("ev", 128, BF), ("od", 128, BF), ("dp", 128, BF), ("dm", 128, BF), ("de", 128, BF), ("do", 128, BF),
        ("s00", 128, F2), ("s01", 128, F2), ("s10", 128, F2), ("s11", 128, F2), ("ut", 512, F2), ("cjf", 512, F2),
        ("q16", 128, BF), ("qm", 128, BF), ("hi", 128, BF), ("nhi", 128, BF), ("ni", 128, BF), ("pi", 128, BF), ("pn", 128, BF),
        ("imf", 128, F2), ("nif", 128, F2), ("nbm", 128, F2), ("b2k", 128, F2), ("bcb", 2048, BF), ("bch", 2048, F2),
        ("gall", 2048, BF), ("gp", 512, BF), ("gn", 512, BF), ("zj", 128, F2), ("zz", 128, F2), ("tlf", 128, F2),
        ("zv", 32, F2), ("vj", 32, U2), ("cvj", 512, U2), ("lv", 128, U2), ("lvi", 128, I4), ("mvi", 128, I4), ("mv", 128, U2),
        ("sf", 512, F2), ("mt_", 8192, BF), ("eqs", 512, BF), ("nh", 512, BF), ("fl", 512, BF), ("wsum", 256, BF),
        ("ok", 256, BF), ("first", 256, F2), ("fz", 256, F2), ("tj", 128, U2), ("tl", 128, U2), ("mint", 512, U2),
        ("eq", 2048, BF), ("inv", 2048, BF), ("lki", 512, I4), ("yli", 128, I4), ("mini", 512, I4), ("ce", 2048, F2),
        ("cj", 2048, U2), ("li", 2048, U2), ("zc", 2048, F2), ("h", 16384, BF), ("part", 2048, BF), ("pin", 3584, BF),
        ("sepin", 2048, U2), ("sepf", 2048, F4), ("rv", 2048, BF), ("mg", 2048, BF), ("rk", 8192, BF), ("xv", 1024, BF),
        ("xy", 1024, BF), ("m", 2048, F4), ("hh", 1024, BF), ("d", 1024 * ND, BF), ("w", 3072, BF), ("s", 3072, BF)):
    SCRATCH[_n] = ("sbuf", [128, _w], _d)
for _n, _w in (("psT", 2048), ("psA", 512), ("psX", 512), ("psW", 1024)):
    SCRATCH[_n] = ("psum", [128, _w], F4)

SEMAPHORES = ["cv", "ca", "cp", "cg", "ltv", "ladj", "lx", "loc", "svj", "slv", "oflag", "brr3"]
for _t in range(NR):
    SEMAPHORES += ["%s%d" % (_k, _t) for _k in ("arr", "sar", "stj", "stl", "mdp", "osep")]
    SEMAPHORES += ["sli%d_%d" % (_t, _k) for _k in range(8)]

CY, GA, SC, PE = 0.9e-3, 1.5, 2.8, 0.43e-3
WAKE, LAT = 0.05, 2.2
LATE = 20.0
LAND = {"arr": 3.0, "sar": 4.0, "brr": 4.0}


def rank_program(g, core, T, topo):
    r = T.rank_of(core)
    if r is None:
        return
    eng = {"v": g.vector, "a": g.scalar, "p": g.tensor, "g": g, "s": g.sync}
    tasks = []
    bonus, lift = {}, [0.0]

    def op(e, fn, reads, writes, cost):
        bonus[len(tasks)] = lift[0]
        tasks.append((e, "op", fn, "c" + e, 1, reads, writes, cost, cost))

    def dma(e, sem, out, in_, reads, writes, lat=LAT, first=0.0):
        bonus[len(tasks)] = first
        tasks.append((e, "dma", lambda q: q.dma_start(out, in_), sem, 16, reads, writes, 0.1, lat))

    def ap(rg):
        return T[rg[0]][:, rg[1]:rg[2]]

    def full(name):
        return (name, 0, SCRATCH[name][1][1])

    def blk(name, k, w=512):
        return (name, w * k, w * k + w)

    def part(rg, q, n=4):
        w = (rg[2] - rg[1]) // n
        return (rg[0], rg[1] + q * w, rg[1] + q * w + w)

    def small(*rgs):
        return all(SCRATCH[x[0]][0] == "sbuf" and SCRATCH[x[0]][2] in (BF, U2, F2) for x in rgs)

    def vc(n, f=1.0):
        return 0.02 + max(64, n * f) * CY

    def copy(e, out, in_):
        n = in_[2] - in_[1]
        if e == "v":
            op("v", lambda q: q.tensor_copy(ap(out), ap(in_)), [in_], [out], vc(n, 0.5 if small(out, in_) else 1))
        else:
            op("a", lambda q: q.activation(ap(out), ap(in_), AF.Copy), [in_], [out], 0.05 + n * CY)

    def act(out, in_, func):
        op("a", lambda q: q.activation(ap(out), ap(in_), func), [in_], [out], 0.05 + (in_[2] - in_[1]) * CY)

    def tt(out, a, b, o):
        f = 1 if a[0].startswith("ps") or b[0].startswith("ps") else 2
        op("v", lambda q: q.tensor_tensor(ap(out), ap(a), ap(b), o), [a, b], [out], vc(a[2] - a[1], f))

    def ts(out, a, s1, o1):
        op("v", lambda q: q.tensor_scalar(ap(out), ap(a), s1, None, o1), [a], [out], vc(a[2] - a[1], 0.5 if small(out, a) else 1))

    def gcost(off):
        return 0.07 + 16 * (off[2] - off[1]) * GA * CY

    def gather(e, out, win, off):
        if e == "v":
            op("v", lambda q: q.tensor_copy(ap(out), ap(win).indirect(ap(off))), [win, off], [out], gcost(off))
        else:
            op("a", lambda q: q.activation(ap(out), ap(win).indirect(ap(off)), AF.Copy), [win, off], [out], gcost(off))

    def gather_less(out, win, off):
        op("v", lambda q: q.tensor_scalar(ap(out), ap(win).indirect(ap(off)), -2048.0, None, OP.add), [win, off], [out], gcost(off))

    def mm(out, lhs, rhs, start, stop, bank=None):
        op("p", lambda q: q.matmul(ap(out), ap(lhs), ap(rhs), start, stop), [lhs, rhs], [bank or out], 0.03 + (rhs[2] - rhs[1]) * PE)

    def gi(i):
        return blk("gall", i, 128)

    def tj(t):
        return blk("tj", t, 32)

    def tl(t):
        return blk("tl", t, 32)

    def li(t, i, n=1):
        return ("li", 512 * t + 32 * i, 512 * t + 32 * i + 32 * n)

    def li3(n, i, k=1):
        return ("li", 1536 + 256 * n + 16 * i, 1536 + 256 * n + 16 * i + 16 * k)

    def hw(t):
        return blk("h", t, 4096)

    def psz(w=512):
        return ("psW", 512, 512 + w)

    XW, AW = full("xs"), full("adjs")

    dma("s", "ltv", T.tvs[:, :], T.tv[:, :], [], [full("tvs")], LAT, 1000.0)
    dma("s", "ladj", T.adjs[:, :], T.adj[:, :], [], [full("adjs")], 7.0, 500.0)
    dma("s", "lx", T.xs[:, 0:4096], T.x[:, :], [], [("xs", 0, 4096)], 10.0, 400.0)

    def fill(rg, val, cost):
        op("v", lambda q: q.memset(ap(rg), val), [], [rg], cost)

    lift[0] = 200.0
    fill(full("ones"), 1.0, 0.1)
    lift[0] = 0.0
    fill(full("bcb"), 1.0, 1.0)
    fill(full("gall"), 0.0, 1.0)
    fill(("xs", 4096, 4112), 0.0, 0.1)

    def asel(out, in_, pat, cmp, base, cm):
        op("g", lambda q: q.affine_select(ap(out), ap(in_), pat, cmp, 0.0, base, cm), [in_], [out], 0.2 + 2 * CY * (in_[2] - in_[1]))

    one128 = full("ones")
    lift[0] = 300.0
    asel(full("c1"), ("ones", 0, 8), [[-16, 8]], OP.is_ge, 0, 1)
    asel(full("c2"), full("c1"), [[16, 8]], OP.is_ge, 15, -1)
    asel(full("im"), one128, [[-1, 128]], OP.is_equal, 0, 1)
    half = [[0, 4], [-1, 2], [0, 16]]
    asel(full("ev"), full("im"), half, OP.is_equal, 0, 0)
    asel(full("od"), full("im"), half, OP.is_equal, 1, 0)
    asel(full("dp"), one128, [[-1, 128]], OP.is_equal, -16, 1)
    asel(full("dm"), one128, [[-1, 128]], OP.is_equal, 16, 1)
    asel(full("de"), full("dp"), half, OP.is_equal, 0, 0)
    asel(full("do"), full("dm"), half, OP.is_equal, 1, 0)
    lift[0] = 250.0
    asel(full("b1"), one128, [[-16, 8], [0, 16]], OP.is_ge, 0, 1)
    asel(full("bm"), full("b1"), [[16, 8], [0, 16]], OP.is_ge, 15, -1)
    asel(full("lt"), full("bm"), [[1, 128]], OP.is_gt, 0, -1)
    lift[0] = 0.0
    asel(full("bcb"), full("bcb"), [[-1, 16], [-16, 8], [0, 16]], OP.is_equal, 0, 1)

    def zeros(s, *after):
        op("g", lambda q: q.iota(ap(hw(s)), [[0, 4096]], 0, 0, allow_small_or_imprecise_dtypes=True), list(after), [hw(s)], 7.0)

    for s in range(2):
        zeros(s, full("lt"))

    def diag(i):
        op("v", lambda q: q.tensor_copy(T.gall[:, 128 * i + i:128 * i + 128:16], T.c2[:, :]), [full("c2")], [gi(i)], 0.12)

    lift[0] = 200.0
    copy("v", full("tvu"), full("tvs"))
    for a, b in (("s00", "ev"), ("s11", "od"), ("s10", "de"), ("s01", "do")):
        copy("v", full(a), full(b))
    lift[0] = 0.0
    for i in range(16):
        diag(i)
    for nm, f in (("hi", 0.5), ("nhi", -0.5), ("ni", -1.0), ("pi", 512.0), ("pn", -512.0), ("imf", 1.0), ("nif", -1.0)):
        ts(full(nm), full("im"), f, OP.mult)
    ts(full("gp"), ("gall", 0, 512), 64.0, OP.mult)
    ts(full("gn"), ("gall", 0, 512), -64.0, OP.mult)

    SEL = [["s00", "s01"], ["s10", "s11"]]

    def flip(rows):
        op("v", lambda q: q.transpose(T.ut[:, :], ap(rows)), [rows], [full("ut")], vc(256))

    def pick(u, h):
        op("p", lambda q: q.matmul(T.psX[:, 16 * u:16 * u + 16], T[SEL[u][h]][:, :], T.ut[:, 16 * h:512:32], h == 0, h == 1),
           [full(SEL[u][h]), full("ut")], [("psX", 0, 32)], 0.06)

    def ylist(u):
        op("v", lambda q: q.tensor_scalar(T.tl[:, u:32:2], T.psX[:, 16 * u:16 * u + 16], 2048.0, None, OP.add),
           [("psX", 0, 32)], [tl(0)], vc(16))

    def ymix(u):
        op("v", lambda q: q.tensor_copy(T.tj[:, u:32:2], T.tl[:, 16 * u:16 * u + 16]), [tl(0)], [tj(0)], vc(16))

    def entry(i):
        op("v", lambda q: q.tensor_scalar(ap(li(0, i)), T.psW[:, i:1024:32], 2048.0, None, OP.add), [full("psW")], [li(0, i)], vc(32))

    def first_lists():
        gather_less(blk("ce", 0), AW, blk("tvu", 0, 32))
        flip(blk("ce", 0))
        for u in range(2):
            for h in range(2):
                pick(u, h)
        for u in range(2):
            ylist(u)
        for u in range(2):
            ymix(u)
        gather_less(full("cjf"), AW, tj(0))
        flip(full("cjf"))
        for u in range(2):
            for h in range(2):
                mm(("psW", 512 * u, 512 * u + 496), full(SEL[u][h]), ("ut", 16 * h, 16 * h + 496), h == 0, h == 1)
        for i in range(1, 16):
            entry(i)

    def rows_v(t):
        a, b = 512 * t, 32 * t
        gather_less(blk("ce", t), AW, blk("tvu", t, 32))
        for n in range(2):
            dma("s", "stj%d" % t, T.zj[:, b + 16 * n:b + 16 * n + 16], T.ce[t::16, a + 256 * n:a + 256 * n + 256],
                [blk("ce", t)], [("zj", b + 16 * n, b + 16 * n + 16)], LAT, 50.0)
        for n in range(2):
            dma("s", "stl%d" % t, T.zz[:, b + 16 * n:b + 16 * n + 16], T.ce[t + 16 * n::32, a:a + 512],
                [blk("ce", t)], [("zz", b + 16 * n, b + 16 * n + 16)], LAT, 40.0)

    def plus(out, a, b, step, src):
        op("v", lambda q: q.tensor_scalar(T[out][:, a:b:step], ap(src), 2048.0, None, OP.add), [src], [(out, a, b)], vc(16))

    def rows_y(t):
        b = 32 * t
        if t == 3:
            plus("tj", b, b + 32, 1, ("zj", b, b + 32))
        else:
            for n in range(2):
                plus("tj", b + n, b + 32, 2, ("zj", b + 16 * n, b + 16 * n + 16))
        gather("v", blk("cj", t), AW, tj(t))
        op("v", lambda q: q.transpose(T.tlf[:, b:b + 32], T.zz[:, b:b + 32]), [("zz", b, b + 32)], [("tlf", b, b + 32)], vc(32))
        plus("tl", b, b + 32, 1, ("tlf", b, b + 32))
        rest = [i for i in range(16) if i != t]
        if t == 3:
            for n in range(2):
                for k, i in enumerate(rest):
                    z = li3(n, i)
                    dma("s", "sli3_%d" % ((15 * n + k) // 4), ap(z), T.cj[i::16, 1536 + 256 * n:1792 + 256 * n], [blk("cj", t)], [z],
                        LAT + 0.12 * k)
            return
        for n, i in enumerate(rest):
            dma("s", "sli%d_%d" % (t, n // 4), ap(li(t, i)), T.cj[i::16, 512 * t:512 * t + 512],
                [blk("cj", t)], [li(t, i)], LAT + 0.12 * n)

    lift[0] = 60.0
    first_lists()
    for fn in (rows_v, rows_y):
        for t in range(1, NR):
            lift[0] = 60.0 - 5 * t
            fn(t)
    lift[0] = 0.0

    def prep(t):
        b = t % 2
        xv, xy, hb = blk("xv", b), blk("xy", b), blk("hh", b)
        gather("a", xv, XW, blk("tvu", t, 32))
        gather("a", xy, XW, tl(t))
        mm(full("psX"), full("hi"), xv, True, False)
        mm(full("psX"), full("hi"), xy, False, True)
        if t == 3:
            for n in range(2):
                m1, m2 = ("m", 1024 + 512 * n, 1280 + 512 * n), ("m", 1280 + 512 * n, 1536 + 512 * n)
                copy("a", m1, ("psX", 256 * n, 256 * n + 256))
                dma("s", "mdp3", ap(m2), ap(m1), [m1], [m2], LAT + 0.3)
        else:
            m1, m2 = blk("m", 2 * b), blk("m", 2 * b + 1)
            copy("a", m1, full("psX"))
            if t:
                dma("s", "mdp%d" % t, ap(m2), ap(m1), [m1], [m2], LAT + 0.6)
            else:
                copy("a", m2, full("psX"))
        mm(full("psX"), full("hi"), xv, True, False)
        mm(full("psX"), full("nhi"), xy, False, True)
        act(hb, full("psX"), AF.Abs)

    def mins(t):
        n = NR if t == r else t + 1
        yl = blk("yli", t, 32)
        copy("v", yl, tl(t))
        tt(blk("mini", 5 * t, 32), blk("tvs", t, 32), yl, OP.min)
        if t == 3:
            for k in range(2):
                b = 384 + 64 * k
                copy("v", ("lki", b, b + 48), li3(k, 0, 3))
                for s in range(3):
                    tt(part(blk("mini", 12 + s, 32), k, 2), ("lki", b + 16 * s, b + 16 * s + 16), part(yl, k, 2), OP.min)
        else:
            for a, b in ((0, t), (t + 1, n)):
                if a < b:
                    copy("v", ("lki", 128 * t + 32 * a, 128 * t + 32 * b), li(t, a, b - a))
                for s in range(a, b):
                    tt(blk("mini", 4 * t + s, 32), blk("lki", 4 * t + s, 32), yl, OP.min)
        copy("v", ("mint", 128 * t, 128 * t + 32 * n), ("mini", 128 * t, 128 * t + 32 * n))

    def cols(t):
        zc, inv, eq, off = blk("zc", t), blk("inv", t), blk("eq", t), tl(t)
        if t not in (r, 3):
            zc, inv, off = part(zc, r), part(inv, r), part(off, r)
        gather_less(zc, AW, off)
        ts(inv, zc, 2048.0, OP.is_equal)
        zq = blk("zc", t)
        if t < 3:
            zq, eq = part(zq, r), part(eq, r)
        z = psz(zq[2] - zq[1])
        mm(z, blk("bch", t, 128), zq, True, True)
        tt(eq, z, zq, OP.is_equal)

    def bigmats():
        copy("v", full("bch"), full("bcb"))
        ts(full("q16"), full("lt"), 16.0, OP.mult)
        ts(full("nbm"), full("bm"), -1.0, OP.mult)
        ts(full("b2k"), full("bm"), 2048.0, OP.mult)
        tt(full("qm"), full("q16"), full("im"), OP.subtract)

    units = []
    for t in range(NR):
        ent = [i for i in range(16) if i != t]
        for c in range(2 if t == 3 else 1):
            us = []
            k = 0
            while k < len(ent):
                n = 2 if (t or k) and k + 1 < len(ent) and ent[k + 1] == ent[k] + 1 else 1
                us.append((t, c, ent[k], n))
                k += n
            for j, u in enumerate(us):
                units.append(u + (j == 0, j == len(us) - 1))
    start = [[n for n, u in enumerate(units) if u[0] == t][0] for t in range(NR)] + [len(units)]

    def unit(n):
        t, ch, i, k, fst, lst = units[n]
        wd = 256 if t == 3 else 512
        c, d0, w0, p0, m0 = wd * k, 1024 * (n % ND), 1024 * (n % 3), 1024 * (n % 2), 1024 * (t % 2) + 512 * ch
        d, w, s, m, off = ("d", d0, d0 + c), ("w", w0, w0 + c), ("s", w0, w0 + c), ("m", m0, m0 + c), li(t, i, k)
        hq, acc = blk("hh", t % 2), full("psA")
        if t == 3:
            off = li3(ch, i, k)
            hq = part(hq, ch, 2)
            acc = ("psX" if ch else "psA", 0, 256)
        op("v", lambda q: q.tensor_tensor(ap(d), ap(XW).indirect(ap(off)), ap(m), OP.subtract), [XW, off, m], [d], gcost(off))
        act(w, d, AF.Abs)
        for j in range(k):
            o = ("psT", p0 + wd * j, p0 + wd * j + wd)
            bank = ("psT", p0, p0 + 512) if t == 3 else o
            mm(o, full("im"), ("w", w0 + wd * j, w0 + wd * j + wd), True, False, bank)
            mm(o, full("ni"), hq, False, True, bank)
        act(s, ("psT", p0, p0 + c), AF.Sign)
        for j in range(k):
            mm(acc, gi(i + j), ("s", w0 + wd * j, w0 + wd * j + wd), fst and j == 0, lst and j == k - 1)

    others = [q for q in range(NR) if q != r]
    links = topo.engines(core, T.cores[others[0]])

    def dst(q):
        a = topo.addr(T.cores[q])
        return DstId(rid=a[0], pnc=a[1])

    def remote(name, t, transfers, nloc, nrem, src, land):
        tasks.append(("g", "send", lambda q: q.remote_dma_fused(transfers, local_sem=T.sem.loc), "loc", nloc, [src],
                      [("token" + name, t, t + 1)], 0.6, 0.6))
        tasks.append((None, "land", None, name + str(t), 3 * nrem, [("token" + name, t, t + 1)], land, 0.0, LAND[name]))

    def share(t):
        mine = blk("part", t)
        copy("a", mine, full("psA"))
        k = len(links) // 4
        tr = []
        for n, q in enumerate(others):
            mask = sum(1 << e for e in links[n * k:n * k + k])
            tr.append(RemoteDMATransfer(dst_ids=[dst(q)], dma_engine_mask=mask, remote_sem=T.sem["arr%d" % t],
                                        srcs=[ap(part(mine, q))], dsts=[ap(part(blk("pin", t), r))]))
        remote("arr", t, tr, 3 * k, k, mine, [part(blk("pin", t), q) for q in others])

    def pin3(q, a, b):
        return ("pin", 1536 + 512 * q + a, 1536 + 512 * q + b)

    def share_all(ch):
        a = 256 * ch
        mine = ("part", 1536 + a, 1792 + a)
        copy("a", mine, ("psX" if ch else "psA", 0, 256))
        name = "brr" if ch else "arr"
        tr = [RemoteDMATransfer(dst_ids=[dst(q) for q in others], dma_engine_mask=topo.mask(core, T.cores[others[0]]),
                                remote_sem=T.sem[name + "3"], srcs=[ap(mine)], dsts=[ap(pin3(r, a, a + 256)) for _ in others])]
        remote(name, 3, tr, len(links), len(links), mine, [pin3(q, a, a + 256) for q in others])

    def rk(t, s):
        return blk("rk", 4 * t + s)

    def mi(t, s):
        return blk("mint", 4 * t + s, 32)

    def look(t, s):
        if t in (r, 3):
            gather("a", rk(t, s), hw(s), mi(t, s))
        else:
            gather("a", part(rk(t, s), r), hw(s), part(mi(t, s), r))

    def decide(t, a, b):
        def cut(rg):
            return (rg[0], rg[1] + a, rg[1] + b)
        w = b - a
        X, W, K, FI, FZ = [(nm, 0, w) for nm in ("psW", "wsum", "ok", "first", "fz")]
        mm(X, full("pi"), cut(blk("eq", t)), True, False)
        mm(X, full("pi"), cut(blk("inv", t)), False, False)
        for s in range(t):
            mm(X, blk("gp", s, 128), cut(rk(t, s)), False, False)
        mm(X, full("im"), cut(blk("part", t)), False, False)
        for q in others:
            mm(X, full("im"), pin3(q, a, b) if t == 3 else part(blk("pin", t), q), False, q == others[-1])
        act(W, X, AF.Abs)
        ts(K, W, 8.0, OP.is_le)
        mm(X, full("qm"), K, True, True)
        ts(FI, X, -1.0, OP.is_equal)
        tt(FZ, FI, cut(blk("zc", t)), OP.mult)
        mm(X, full("b2k"), FI, True, False)
        mm(X, full("nbm"), FZ, False, True)
        mine = cut(blk("sepin", t))
        copy("v", mine, X)
        if t == 3:
            return
        tr = [RemoteDMATransfer(dst_ids=[dst(q) for q in others], dma_engine_mask=topo.mask(core, T.cores[others[0]]),
                                remote_sem=T.sem["sar%d" % t], srcs=[ap(mine)], dsts=[ap(mine) for _ in others])]
        remote("sar", t, tr, len(links), len(links), mine, [part(blk("sepin", t), q) for q in others])

    def mark(t, a, b):
        if t == 3 and r == 3:
            return
        off, src = ("mint", 160 * t + a // 16, 160 * t + b // 16), ("sepin", 512 * t + a, 512 * t + b)
        op("v", lambda q: q.tensor_copy(ap(hw(t)).indirect(ap(off)), ap(src)), [off, src], [hw(t)], 0.07 + (b - a) * SC * CY)

    def seps(t, a, b):
        a, b = 512 * t + a, 512 * t + b
        out, src = ("sepf", a, b), ("sepin", a, b)
        op("v", lambda q: q.tensor_scalar(ap(out), ap(src), -1.0, 4096.0, OP.mult, OP.add), [src], [out], vc(b - a))
        dma("s", "osep%d" % t, T.ysep[:, a:b], T.sepf[0::16, a:b], [out], [])

    def mj(j):
        return blk("mt_", j)

    def fl_lists():
        for n in range(2):
            dma("s", "svj", T.zv[:, 16 * n:16 * n + 16], T.zc[r::16, 512 * r + 256 * n:512 * r + 256 * n + 256],
                [blk("zc", r)], [("zv", 16 * n, 16 * n + 16)])
        for n in range(2):
            plus("vj", n, 32, 2, ("zv", 16 * n, 16 * n + 16))
        gather("v", full("cvj"), AW, full("vj"))
        for s in range(NR):
            dma("s", "slv", ap(blk("lv", s, 32)), T.cvj[s::16, :], [full("cvj")], [blk("lv", s, 32)])
        copy("v", full("lvi"), full("lv"))
        for s in range(NR):
            if s != r:
                tt(blk("mvi", s, 32), blk("lvi", s, 32), blk("tvs", r, 32), OP.min)
        for a, b in ((0, r), (r + 1, NR)):
            if a < b:
                copy("v", ("mv", 32 * a, 32 * b), ("mvi", 32 * a, 32 * b))

    def match(j):
        mm(psz(), blk("bch", j, 128), blk("ce", r), True, True)
        tt(mj(j), psz(), blk("zc", r), OP.is_equal)

    def fl_own(a, b):
        src, sf, z = ("sepin", 512 * r + a, 512 * r + b), ("sf", a, b), psz(b - a)
        op("v", lambda q: q.tensor_scalar(ap(sf), ap(src), -1.0, 2048.0, OP.mult, OP.add), [src], [sf], vc((b - a) / 2))
        mm(z, full("imf"), sf, True, False)
        mm(z, full("nif"), ("zc", 512 * r + a, 512 * r + b), False, True)
        ts(("eqs", a, b), z, 0.0, OP.is_equal)
        ts(("nh", a, b), src, 0.0, OP.is_equal)

    def fl_gather(s):
        if s != r:
            gather("v", blk("rv", s), hw(s), blk("mv", s, 32))
            if s > r:
                look(r, s)

    def fl_round(s):
        if s != r:
            mm(psz(), full("im"), mj(s), True, s == 3)
            if s == 3:
                tt(blk("mg", s), psz(), blk("rv", s), OP.is_gt)
            else:
                mm(psz(), full("ni"), blk("rv", s), False, True)
                act(blk("mg", s), psz(), AF.Relu)
            mm(F, full("im"), blk("mg", s), False, s == 3)
            if s != 3:
                mm(F, blk("gn", s, 128), rk(r, s), False, False)

    F = full("psA")
    mine = (128 * r, 128 * r + 128)
    for t in range(NR):
        lift[0] = 20.0 if t else 60.0
        prep(t)
        lift[0] = 0.0
        if t == 0:
            bigmats()
            cols(r)
            for k in range(NR):
                mins(k)
                if k != r:
                    cols(k)
        for n in range(start[t + 1] - start[t]):
            unit(start[t] + n)
            if t and n == 2:
                for s in range(t - 1):
                    look(t, s)
                decide(t - 1, *mine)
            if t and n == 5:
                mark(t - 1, 0, 512)
                look(t, t - 1)
                seps(t - 1, 0, 512)
                fl_gather(t - 1)
            if units[start[t] + n][5] and t == 3:
                share_all(units[start[t] + n][1])
        if t == 0:
            fl_lists()
            lift[0] = LATE
            for j in range(16):
                if j != r:
                    match(j)
            lift[0] = 0.0
        if t < 3:
            share(t)
        if t == 0:
            for s in range(2, NR if r != 3 else 3):
                zeros(s, ("tokenarr", 0, 1))
    mm(F, full("pn"), blk("inv", r), True, False)
    for j in range(4, 16):
        mm(F, full("im"), mj(j), False, False)
    for s in range(3):
        if s != r:
            fl_round(s)
    if r != 3:
        fl_own(0, 512)
        mm(F, full("pn"), full("eqs"), False, False)
        mm(F, full("pn"), full("nh"), False, False)
    for c in range(2):
        a, b = 256 * c, 256 * c + 256
        decide(3, a, b)
        mark(3, a, b)
        seps(3, a, b)
        if r == 3:
            fl_own(a, b)
    if r != 3:
        fl_gather(3)
        mm(F, blk("gn", 3, 128), rk(r, 3), False, False)
        fl_round(3)
    else:
        mm(F, full("pn"), full("nh"), False, False)
        mm(F, full("pn"), full("eqs"), False, True)
    ts(full("fl"), F, 0.0, OP.is_gt)
    dma("s", "oflag", T.yflag[:, :], T.fl[:, :], [full("fl")], [])

    cnt, snap, recs = {}, {}, {}
    clock = {e: {} for e in eng}

    def wait(e, sem, val, isdma):
        if isdma:
            val = cnt[sem]
        if clock[e].get(sem, 0) >= val:
            return
        eng[e].wait_ge(T.sem[sem], val)
        for k, v in snap.get(sem if isdma else (sem, val), {}).items():
            if clock[e].get(k, 0) < v:
                clock[e][k] = v
        clock[e][sem] = max(clock[e].get(sem, 0), val)

    for x in schedule(tasks, bonus):
        e, kind, fn, sem, inc, reads, writes, _, _ = tasks[x]
        reads = [q for q in reads if not q[0].startswith("token")]
        writes = [q for q in writes if not q[0].startswith("token")]
        isdma = kind != "op"
        if kind != "land":
            best = {}
            for isw, rgs in ((False, reads), (True, writes)):
                for buf, a, b in rgs:
                    for c0, c1, w, e2, s2, v2, d2 in recs.get(buf, []):
                        if c0 >= b or a >= c1:
                            continue
                        if not isw and not w and not (buf.startswith("ps") and e2 != e):
                            continue
                        if isw and e2 == e and not d2 and not isdma and (not w or e == "p"):
                            continue
                        if s2 not in best or best[s2][0] < v2:
                            best[s2] = (v2, d2)
            for s2 in sorted(best, key=lambda z: (best[z][1], z)):
                wait(e, s2, best[s2][0], best[s2][1])
        cnt[sem] = cnt.get(sem, 0) + inc
        if kind == "send":
            fn(eng[e])
            continue
        if kind != "land":
            fn(eng[e]).then_inc(T.sem[sem], inc)
            if kind == "op":
                sn = dict(clock[e])
                sn[sem] = cnt[sem]
                snap[(sem, cnt[sem])] = sn
            else:
                sn = snap.setdefault(sem, {})
                for k, v in clock[e].items():
                    sn[k] = max(sn.get(k, 0), v)
        for buf, a, b in writes:
            lst = recs.setdefault(buf, [])
            lst[:] = [q for q in lst if not (a <= q[0] and q[1] <= b)]
            lst.append((a, b, True, e, sem, cnt[sem], isdma))
        for buf, a, b in reads:
            lst = recs.setdefault(buf, [])
            lst[:] = [q for q in lst if not (not q[2] and q[4] == sem and a <= q[0] and q[1] <= b)]
            lst.append((a, b, False, e, sem, cnt[sem], isdma))

    for sem, val in cnt.items():
        if clock["g"].get(sem, 0) < val:
            g.wait_ge(T.sem[sem], val)
            clock["g"][sem] = val


def schedule(tasks, bonus):
    n = len(tasks)
    deps = [set() for _ in range(n)]
    recs, group = {}, {}
    for x in range(n):
        e, kind, _, sem, _, reads, writes, _, _ = tasks[x]
        for isw, rgs in ((False, reads), (True, writes)):
            for buf, a, b in rgs:
                for c0, c1, w, e2, y in recs.get(buf, []):
                    if c0 < b and a < c1 and (isw or w or (buf.startswith("ps") and e2 != e)):
                        deps[x].add(y)
        for y in list(deps[x]):
            if tasks[y][1] == "dma":
                deps[x].update(z for z in group[tasks[y][3]] if z < x)
        if kind == "dma":
            group.setdefault(sem, []).append(x)
        for buf, a, b in writes:
            lst = recs.setdefault(buf, [])
            lst[:] = [q for q in lst if not (a <= q[0] and q[1] <= b)]
            lst.append((a, b, True, e, x))
        for buf, a, b in reads:
            recs.setdefault(buf, []).append((a, b, False, e, x))
        deps[x].discard(x)
    succ = [[] for _ in range(n)]
    for x in range(n):
        for y in deps[x]:
            succ[y].append(x)
    prio = [0.0] * n
    for x in range(n - 1, -1, -1):
        prio[x] = tasks[x][8] + WAKE + max([prio[y] for y in succ[x]], default=0.0)
    prio = [prio[x] + bonus.get(x, 0.0) for x in range(n)]
    left = [len(deps[x]) for x in range(n)]
    at = [0.0] * n
    free = {}
    ready = {}
    for x in range(n):
        if not left[x]:
            ready.setdefault(tasks[x][0], []).append(x)
    order = []
    while len(order) < n:
        pick = None
        for e in sorted(ready, key=str):
            lst = ready[e]
            if not lst:
                continue
            f = free.get(e, 0.0)
            s0 = min(max(f, at[x]) for x in lst)
            if pick is None or s0 < pick[0]:
                pick = (s0, e)
        s0, e = pick
        x = max((y for y in ready[e] if max(free.get(e, 0.0), at[y]) <= s0 + 0.05), key=lambda y: (prio[y], -y))
        ready[e].remove(x)
        st = max(free.get(e, 0.0), at[x])
        if e is not None:
            free[e] = st + tasks[x][7]
        end = st + tasks[x][8] + WAKE
        order.append(x)
        for y in succ[x]:
            at[y] = max(at[y], end)
            left[y] -= 1
            if not left[y]:
                ready.setdefault(tasks[y][0], []).append(y)
    return order
